import numpy as np
import ml_dtypes


def mxq(x, axis, fmt="e4m3"):
    dtype, down = {"e4m3": (ml_dtypes.float8_e4m3fn, 7), "e5m2": (ml_dtypes.float8_e5m2, 14)}[fmt]
    v = np.moveaxis(np.asarray(x, np.float32).astype(ml_dtypes.bfloat16).astype(np.float64), axis, -1)
    blocks = v.reshape(v.shape[:-1] + (-1, 32))
    amax = np.abs(blocks).max(-1, keepdims=True)
    byte = np.maximum(np.where(amax > 0, np.frexp(amax)[1] - 1 + 127, 0) - down, 1)
    scale = np.exp2(byte - 127.0)
    codes = (blocks / scale).astype(np.float32).astype(dtype).astype(np.float64)
    return np.moveaxis((codes * scale).reshape(v.shape), -1, axis)


WIDE = False


def mx_kscale(k):
    if not WIDE:
        return np.ones(k)
    levels = np.array([10, -10, 5, -5, 0])
    if k % 512:
        return np.exp2(np.random.permutation(np.resize(levels, k // 32))).repeat(32)
    a = np.empty((k // 512, 16))
    for p in range(k // 512):
        a[p, :8] = np.random.permutation(np.resize(levels, 8))
        for g in range(8):
            far = levels[np.abs(levels - a[p, g]) >= 10]
            a[p, g + 8] = far[np.random.randint(len(far))]
    return np.exp2(a.ravel()).repeat(32)


BF16 = ml_dtypes.bfloat16


def bf(x):
    return np.asarray(x, np.float32).astype(BF16)


def f64(x):
    return np.asarray(x).astype(np.float64)


E2M1 = np.array([0.0, 0.5, 1.0, 1.5, 2.0, 3.0, 4.0, 6.0, -0.0, -0.5, -1.0, -1.5, -2.0, -3.0, -4.0, -6.0])


def pack_weight(w, fmt):
    k, n = w.shape
    w = f64(bf(w)).reshape(k // 32, 32, n)
    amax = np.abs(w).max(1)
    if fmt == "e4m3":
        byte = np.frexp(amax)[1] - 1 + 127 - 7
    else:
        mant, ex = np.frexp(amax / 6.0)
        byte = np.where(mant > 0.5, ex, ex - 1) + 127
    byte = np.clip(np.where(amax > 0, byte, 1), 1, 254)
    scaled = (w * np.exp2(127.0 - byte)[:, None, :]).reshape(k, n).astype(np.float32)
    by_word = np.ascontiguousarray(scaled.reshape(k // 512, 128, 4, n).transpose(0, 1, 3, 2))
    if fmt == "e4m3":
        words = by_word.astype(ml_dtypes.float8_e4m3fn).view(np.uint8)
    else:
        c = by_word.astype(ml_dtypes.float4_e2m1fn).view(np.uint8) & 0xF
        words = c[..., 0::2] | (c[..., 1::2] << 4)
    return np.ascontiguousarray(words), np.ascontiguousarray(byte.astype(np.uint8).reshape(k // 512, 16, n))


def unpack_weight(words, scales, fmt):
    g, p, n, _ = words.shape
    if fmt == "e4m3":
        vals = np.ascontiguousarray(words).view(ml_dtypes.float8_e4m3fn).astype(np.float64)
    else:
        nib = np.empty((g, p, n, 4), np.uint8)
        nib[..., 0::2] = words & 0xF
        nib[..., 1::2] = words >> 4
        vals = E2M1[nib]
    vals = vals * np.repeat(np.exp2(scales.astype(np.float64) - 127.0), 8, axis=1)[..., None]
    return vals.transpose(0, 1, 3, 2).reshape(g * 512, n)
def pack4(w):
    words, scales = pack_weight(w, "e2m1")
    return words.reshape(words.shape[0], 128, -1), scales


def unpack4(words, scales):
    return unpack_weight(words.reshape(words.shape[0], 128, -1, 2), scales, "e2m1")


S, T, F, C = 512, 4, 1024, 512

BLEED = 0.35


def setup_inputs():
    s = mx_kscale(S)
    t = mx_kscale(F)
    a = BLEED * np.random.standard_normal((S, S)) / np.sqrt(S) / s[:, None]
    l = BLEED * np.random.standard_normal((F, F)) / np.sqrt(F) / t[:, None] * t
    m = np.random.standard_normal((S, C)) / np.sqrt(S) / s[:, None]
    a_words, a_scales = pack4(a)
    l_words, l_scales = pack4(l)
    m_words, m_scales = pack4(m)
    return {"x": bf(np.random.standard_normal((S, T, F)) * s[:, None, None] * t),
            "a_words": a_words, "a_scales": a_scales,
            "l_words": l_words, "l_scales": l_scales,
            "m_words": m_words, "m_scales": m_scales,
            "damp": bf((1 + 0.1 * np.random.standard_normal(S)) * s),
            "resp": bf((1 + 0.1 * np.random.standard_normal(F)) / t),
            "rec": bf(0.5 * np.random.standard_normal((C, T, F)))}


def reference(x, a_words, a_scales, l_words, l_scales, m_words, m_scales, damp, resp, rec):
    A = unpack4(a_words, a_scales)
    L = unpack4(l_words, l_scales)
    M = unpack4(m_words, m_scales)
    x0 = f64(x).reshape(S, T * F)
    b = A.T @ mxq(x0, 0, "e4m3")
    y = (x0 + f64(damp)[:, None] * b).reshape(S * T, F)
    z = y + (mxq(y, 1, "e4m3") @ L)
    v = (M.T @ mxq(z.reshape(S, T * F), 0, "e4m3")).reshape(C, T, F)
    return v * f64(resp) + f64(rec)

@@ -1,0 +1,308 @@
+from contextlib import ExitStack
+
+import concourse.mybir as mybir
+from concourse.masks import make_identity
+
+F32 = mybir.dt.float32
+BF16 = mybir.dt.bfloat16
+U32 = mybir.dt.uint32
+I32 = mybir.dt.int32
+U8 = mybir.dt.uint8
+E4M3 = mybir.dt.float8_e4m3fn_x4
+E2M1 = mybir.dt.float4_e2m1fn_x4
+ADD = mybir.AluOpType.add
+MULT = mybir.AluOpType.mult
+
+S, T, F, C = 512, 4, 1024, 512
+P = 128
+W = 512
+FLOPS = 2 * (2 * S * S * T * F + S * T * F * F)
+
+ACC_BUFS = 6
+TR_BUFS = 2
+COPY = mybir.ActivationFunctionType.Copy
+INTER = "bbvsssss"
+E_OFF = ()
+J_OFF = ()
+V_ADD = ((7,0),(7,2),(6,2))
+
+
+def tile_orchestra_bleed_mix_t2_kernel(
+    tc, x, a_words, a_scales, l_words, l_scales, m_words, m_scales, damp, resp, rec, out
+):
+    nc = tc.nc
+    with ExitStack() as ctx:
+        keep = ctx.enter_context(tc.tile_pool(name="keep", bufs=1))
+        work = ctx.enter_context(tc.tile_pool(name="work", bufs=3))
+        psum = ctx.enter_context(tc.psum_pool(name="psum", bufs=1))
+        ctx.enter_context(tc.manual_schedule())
+
+        a_raw = keep.tile([P, 1024], U8, align_bytes=64)
+        a_sraw = keep.tile([P, 512], U8, align_bytes=64)
+        a_cod = keep.tile([P, 1024], U8, align_bytes=64)
+        a_sc = keep.tile([P, 4, P], U8, align_bytes=64)
+        l_cod = keep.tile([P, 2, 2 * F], U8, align_bytes=64)
+        l_sc = keep.tile([P, 2, F], U8, align_bytes=64)
+        m_cod = keep.tile([P, 2 * C], U8, align_bytes=64)
+        m_sc = keep.tile([P, C], U8, align_bytes=64)
+        damp_t = keep.tile([P, 4], BF16)
+        resp_t = keep.tile([P, F], BF16, align_bytes=64)
+        rec_t = keep.tile([P, 4, T, F], BF16, align_bytes=64)
+        ident = keep.tile([P, P], F32, align_bytes=64)
+
+        def words(tile):
+            return tile.bitcast(I32)
+
+        nc.vector.memset(words(a_sraw[:]), 0)
+        nc.vector.memset(words(l_sc[:]), 0)
+        nc.vector.memset(words(m_sc[:]), 0)
+        make_identity(nc, ident[:])
+
+        raws = []
+        for r in range(T):
+            raw = keep.tile([P, 4, F], BF16, align_bytes=64, name="raw%d" % r)
+            raws.append(raw)
+
+        def load_x(r, f0, f1):
+            nc.sync.dma_start(out=raws[r][:, :, f0:f1], in_=x.rearrange("(p j) r f -> p j r f", j=4)[:, :, r, f0:f1])
+
+        nc.sync.dma_start(out=words(a_raw[:]), in_=words(a_words[0]))
+        for q in range(4):
+            nc.sync.dma_start(out=words(a_sraw[32 * q : 32 * q + 4, :]), in_=words(a_scales[0, 4 * q : 4 * q + 4, :]))
+        nc.sync.dma_start(out=damp_t[:], in_=damp.rearrange("(p t) -> p t", t=4))
+        load_x(0, 0, W)
+        load_x(0, W, F)
+        load_x(1, 0, F)
+        nc.sync.dma_start(out=words(l_cod[:]), in_=words(l_words.rearrange("g p n -> p g n")))
+        for q in range(4):
+            nc.sync.dma_start(
+                out=words(l_sc[32 * q : 32 * q + 4, :, :]),
+                in_=words(l_scales[:, 4 * q : 4 * q + 4, :].rearrange("g q n -> q g n")),
+            )
+        load_x(2, 0, F)
+        nc.sync.dma_start(out=words(m_cod[:]), in_=words(m_words[0]))
+        for q in range(4):
+            nc.sync.dma_start(out=words(m_sc[32 * q : 32 * q + 4, :]), in_=words(m_scales[0, 4 * q : 4 * q + 4, :]))
+        nc.sync.dma_start(out=resp_t[:], in_=resp.partition_broadcast(P))
+        rec_v = rec.rearrange("(m c) r f -> c m r f", c=P)
+        nc.sync.dma_start(out=rec_t[:, :, 0, :], in_=rec_v[:, :, 0, :])
+        load_x(3, 0, F)
+        for r in range(1, T):
+            nc.sync.dma_start(out=rec_t[:, :, r, :], in_=rec_v[:, :, r, :])
+
+        damp_f = keep.tile([P, 4], F32)
+
+        nc.vector.tensor_copy(out=a_cod[:].rearrange("p (t m b) -> p t m b", t=4, b=2), in_=a_raw[:].rearrange("p (m t b) -> p t m b", t=4, b=2))
+        nc.vector.tensor_copy(out=a_sc[:], in_=a_sraw[:].rearrange("p (m t) -> p t m", t=4))
+
+        xg, xc, xs = {}, {}, {}
+        y, yt, yc, ys = {}, {}, {}, {}
+        z, zc, zs = {}, {}, {}
+        acc, tr = {}, {}
+
+        def interleave(u, engine, c0, c1):
+            r, g = divmod(u, 2)
+            if u not in xg:
+                xg[u] = work.tile([P, W, 4], BF16, align_bytes=64, name="xg")
+            o = xg[u][:, c0:c1, :].rearrange("p (c i) t -> p c t i", i=4)
+            i_ = raws[r][:, :, g * W + c0 : g * W + c1].rearrange("p t (c i) -> p c t i", i=4)
+            if engine == "v":
+                nc.vector.tensor_copy(out=o, in_=i_)
+            elif engine == "g":
+                nc.gpsimd.tensor_scalar(out=o, in0=i_, scalar1=1.0, scalar2=0.0, op0=MULT, op1=ADD)
+            else:
+                nc.scalar.copy(out=o, in_=i_)
+
+        def quant_x(u):
+            xc[u] = work.tile([P, W], U32, align_bytes=64, name="xc")
+            xs[u] = work.tile([P, W], U8, align_bytes=64, name="xs")
+            nc.vector.quantize_mx(
+                out=xc[u][:].bitcast(E4M3), scales=xs[u][:], in_=xg[u][:].rearrange("p w t -> p (w t)")
+            )
+
+        def mm1(u, t):
+            bank = psum.tile([P, W], F32, name="acc", bufs=ACC_BUFS)
+            acc["E", u, t] = bank
+            nc.tensor.matmul_mx(
+                out=bank[:],
+                lhsT=a_cod[:, 2 * P * t : 2 * P * (t + 1)].bitcast(E2M1),
+                lhsT_scale=a_sc[:, t, :],
+                rhs=xc[u][:].bitcast(E4M3),
+                rhs_scale=xs[u][:],
+                start=True,
+                stop=True,
+            )
+
+        def bleed(u, t):
+            r, g = divmod(u, 2)
+            if r not in y:
+                y[r] = work.tile([P, 4, 2, 4, P], F32, align_bytes=64, name="y")
+            if (u, t) in E_OFF:
+                et = work.tile([P, 4, P], F32, name="et", bufs=2)
+                nc.scalar.activation(
+                    out=et[:], in_=acc["E", u, t][:].rearrange("p (m s) -> p s m", s=4), func=COPY, scale=damp_f[:, t : t + 1]
+                )
+                nc.gpsimd.tensor_tensor(
+                    out=y[r][:, t, g, :, :],
+                    in0=et[:],
+                    in1=raws[r][:, t, g * W : (g + 1) * W].rearrange("p (m s) -> p s m", s=4),
+                    op=ADD,
+                )
+                return
+            nc.vector.scalar_tensor_tensor(
+                out=y[r][:, t, g, :, :],
+                in0=acc["E", u, t][:].rearrange("p (m s) -> p s m", s=4),
+                scalar=damp_t[:, t : t + 1],
+                in1=raws[r][:, t, g * W : (g + 1) * W].rearrange("p (m s) -> p s m", s=4),
+                op0=MULT,
+                op1=ADD,
+            )
+
+        def turn(u, t):
+            r, g = divmod(u, 2)
+            bank = psum.tile([P, 4, P], F32, name="tr", bufs=TR_BUFS)
+            for s in range(4):
+                nc.tensor.transpose(bank[:, s, :], y[r][:, t, g, s, :], ident[:])
+            if u not in yt:
+                yt[u] = work.tile([P, 512, 4], BF16, align_bytes=64, name="yt")
+            nc.scalar.copy(out=yt[u][:, t * P : (t + 1) * P, :], in_=bank[:].rearrange("p s j -> p j s"))
+
+        def quant_y(u):
+            yc[u] = work.tile([P, 512], U32, align_bytes=64, name="yc", bufs=4)
+            ys[u] = work.tile([P, 512], U8, align_bytes=64, name="ys", bufs=4)
+            nc.vector.quantize_mx(
+                out=yc[u][:].bitcast(E4M3), scales=ys[u][:], in_=yt[u][:].rearrange("p j s -> p (j s)")
+            )
+
+        def mm2(r, b):
+            bank = psum.tile([P, 4, P], F32, name="acc", bufs=ACC_BUFS)
+            acc["J", r, b] = bank
+            for t in range(4):
+                for g in range(2):
+                    u = 2 * r + g
+                    nc.tensor.matmul_mx(
+                        out=bank[:, t, :],
+                        lhsT=yc[u][:, t * P : (t + 1) * P].bitcast(E4M3),
+                        lhsT_scale=ys[u][:, t * P : (t + 1) * P],
+                        rhs=l_cod[:, g, 2 * P * b : 2 * P * (b + 1)].bitcast(E2M1),
+                        rhs_scale=l_sc[:, g, P * b : P * (b + 1)],
+                        start=(g == 0),
+                        stop=(g == 1),
+                    )
+
+        def leak(r, b):
+            g, bb = divmod(b, 4)
+            v = 2 * r + g
+            if v not in z:
+                z[v] = work.tile([P, 4, P, 4], BF16, align_bytes=64, name="z")
+            ms = slice(32 * bb, 32 * bb + 32)
+            if (v, bb) in J_OFF:
+                jt = work.tile([P, 4, P], F32, name="jt", bufs=2)
+                nc.scalar.copy(out=jt[:], in_=acc["J", r, b][:])
+                nc.gpsimd.tensor_tensor(
+                    out=z[v][:, :, ms, :],
+                    in0=jt[:].rearrange("p t (m s) -> p s m t", s=4),
+                    in1=y[r][:, :, g, :, ms].rearrange("p t s m -> p s m t"),
+                    op=ADD,
+                )
+                return
+            nc.vector.tensor_tensor(
+                out=z[v][:, :, ms, :],
+                in0=acc["J", r, b][:].rearrange("p t (m s) -> p s m t", s=4),
+                in1=y[r][:, :, g, :, ms].rearrange("p t s m -> p s m t"),
+                op=ADD,
+            )
+
+        def quant_z(v):
+            zc[v] = work.tile([P, W], U32, align_bytes=64, name="zc")
+            zs[v] = work.tile([P, W], U8, align_bytes=64, name="zs")
+            nc.vector.quantize_mx(
+                out=zc[v][:].bitcast(E4M3), scales=zs[v][:], in_=z[v][:].rearrange("p s m t -> p (s m t)")
+            )
+
+        def mm3(v, m):
+            bank = psum.tile([P, W], F32, name="acc", bufs=ACC_BUFS)
+            acc["M", v, m] = bank
+            nc.tensor.matmul_mx(
+                out=bank[:],
+                lhsT=m_cod[:, 2 * P * m : 2 * P * (m + 1)].bitcast(E2M1),
+                lhsT_scale=m_sc[:, P * m : P * (m + 1)],
+                rhs=zc[v][:].bitcast(E4M3),
+                rhs_scale=zs[v][:],
+                start=True,
+                stop=True,
+            )
+
+        def mix(v, m):
+            r, g = divmod(v, 2)
+            fs = slice(g * W, (g + 1) * W)
+            res = work.tile([P, W], F32, name="res", bufs=4)
+            nc.vector.tensor_tensor(
+                out=res[:].rearrange("p (m s) -> p m s", s=4),
+                in0=acc["M", v, m][:].rearrange("p (s m) -> p m s", s=4),
+                in1=resp_t[:, fs].rearrange("p (m s) -> p m s", s=4),
+                op=MULT,
+            )
+            fin = work.tile([P, W], F32, name="fin", bufs=6)
+            add_engine = nc.vector if (v, m) in V_ADD else nc.gpsimd
+            add_engine.tensor_tensor(out=fin[:], in0=res[:], in1=rec_t[:, m, r, fs], op=ADD)
+            nc.sync.dma_start(out=out[m * P : (m + 1) * P, r, fs], in_=fin[:])
+
+        order = [("Qx", 0)]
+        late = []
+        for h in range(11):
+            e = [("E", h, t) for t in range(4)] if h < 8 else []
+            m = [("M", h - 3, k) for k in range(4)] if 0 <= h - 3 < 8 else []
+            j = [("J",) + ((h - 2) // 2, 4 * ((h - 2) % 2) + k) for k in range(4)] if 0 <= h - 2 < 8 else []
+            qz = [("Qz", h - 3)] if 0 <= h - 3 < 8 else []
+            qy = [("Qy", h - 1)] if 0 <= h - 1 < 8 else []
+            if h < 8:
+                order += e[0:1] + qz + e[1:2] + qy + e[2:3] + m[0:2] + e[3:4] + m[2:4]
+                if h < 7:
+                    order += [("Qx", h + 1)]
+                order += j
+            elif h == 8:
+                order += qz + m[0:2] + qy + m[2:4] + j[0:4]
+            elif h == 9:
+                order += j[0:1] + qz + j[1:4] + m[0:2]
+                late = m[2:4]
+            else:
+                order += qz + late + m
+
+        banks = [i for i in range(len(order)) if order[i][0] in ("E", "J", "M")]
+        make = {"E": mm1, "J": mm2, "M": mm3}
+        use = {"E": bleed, "J": leak, "M": mix, "Qx": quant_x, "Qy": quant_y, "Qz": quant_z}
+        feeds = {"E": lambda k: ("Qx", k[1]), "J": lambda k: ("Qy", 2 * k[1] + 1), "M": lambda k: ("Qz", k[1])}
+
+        def inter(u):
+            if u < T * 2:
+                if INTER[u] == "b":
+                    interleave(u, "s", 256, 512)
+                    interleave(u, "v", 0, 256)
+                else:
+                    interleave(u, INTER[u], 0, W)
+
+        inter(0)
+        nc.vector.tensor_copy(out=damp_f[:], in_=damp_t[:])
+        done = set()
+        filled = 0
+        turns = []
+        for i in range(len(order)):
+            op = order[i]
+            ahead = len([b for b in banks if b < i]) + ACC_BUFS
+            while filled < min(ahead, len(banks)):
+                nxt = order[banks[filled]]
+                if feeds[nxt[0]](nxt) not in done:
+                    break
+                make[nxt[0]](*nxt[1:])
+                filled += 1
+            use[op[0]](*op[1:])
+            done.add(op)
+            if op[0] == "Qx":
+                inter(op[1] + 1)
+            if op[0] == "E":
+                turns.append(op[1:])
+            if len(turns) >= 2 and op[0] != "E" or len(turns) == 3:
+                for w in turns[:2]:
+                    turn(*w)
+                turns = turns[2:]

@@ -20,11 +20,8 @@ FLOPS = 2 * (2 * S * S * T * F + S * T * F * F)
 
 ACC_BUFS = 6
 TR_BUFS = 2
+PROG = """A Is,0,256,512 Iv,0,0,256 Iv,1,0,256 Is,1,256,512 Qx,0 Iv,2,0,512 S1,0,0 S1,0,1 S1,0,2 S1,0,3 E,0,0 Qx,1 R,0,0 E,0,1 S1,1,0 S1,1,1 E,0,2 R,0,1 S1,1,2 S1,1,3 E,0,3 R,0,2 T,0,0 E,1,0 R,0,3 Qx,2 G,0,0 T,0,2 E,1,1 R,1,0 S1,2,0 S1,2,1 E,1,2 G,0,2 S1,2,2 S1,2,3 E,1,3 R,1,1 Qy,0 R,1,2 T,1,0 Iv,3,0,512 R,1,3 G,1,0 T,1,2 Is,4,0,128 E,2,0 G,1,2 Qx,3 R,2,0 Qy,1 S1,3,0 Is,4,128,256 S1,3,1 E,2,1 S2,0,0 Is,4,256,384 E,2,2 S2,0,1 E,2,3 R,2,1 S2,0,2 J,0,0 R,2,2 S2,0,3 J,0,1 R,2,3 S1,3,2 J,0,2 Is,4,384,512 S1,3,3 J,0,3 T,2,0 Is,5,0,128 E,3,0 T,2,2 G,2,0 Qz,0 S2,1,0 G,2,2 Qx,4 S2,1,1 R,3,0 Qy,2 Is,5,128,256 S3,0,0 E,3,1 Is,5,256,384 M,0,0 S3,0,1 R,3,1 M,0,1 S3,0,2 Ng,0,0 Is,5,384,512 T,3,0 M,0,2 Is,6,0,128 E,3,2 S3,0,3 Ng,0,1 S2,1,2 M,0,3 G,3,0 S2,1,3 E,3,3 R,3,2 Ng,0,2 S1,4,0 J,1,0 Is,6,128,256 S1,4,1 J,1,1 S1,4,2 R,3,3 Ng,0,3 J,1,2 S1,4,3 Is,6,256,384 T,3,2 J,1,3 Is,6,384,512 E,4,0 G,3,2 Qz,1 R,4,0 Qy,3 S3,1,0 Is,7,0,128 S3,1,1 Qx,5 S3,1,2 Is,7,128,256 M,1,0 Is,7,256,384 M,1,1 S3,1,3 Ng,1,0 Is,7,384,512 M,1,2 S2,2,0 M,1,3 Ng,1,1 S2,2,1 E,4,1 S2,2,2 E,4,2 R,4,1 Ng,1,2 S2,2,3 E,4,3 R,4,2 S1,5,0 J,2,0 S1,5,1 R,4,3 Ng,1,3 T,4,0 J,2,1 T,4,2 J,2,2 G,4,0 J,2,3 S1,5,2 G,4,2 S1,5,3 E,5,0 S2,3,0 Qy,4 S2,3,1 R,5,0 Qz,2 S2,3,2 Qx,6 E,5,1 E,5,2 R,5,1 S3,2,0 M,2,0 S3,2,1 R,5,2 T,5,0 M,2,1 Ng,2,0 E,5,3 S3,2,2 G,5,0 S3,2,3 M,2,2 R,5,3 S2,3,3 Ng,2,1 M,2,3 S1,6,0 T,5,2 J,3,0 Ng,2,2 J,3,1 S1,6,1 G,5,2 S1,6,2 J,3,2 S1,6,3 Ng,2,3 Qy,5 J,3,3 S2,4,0 E,6,0 S2,4,1 Qz,3 R,6,0 S2,4,2 Qx,7 E,6,1 E,6,2 R,6,1 S3,3,0 M,3,0 S3,3,1 R,6,2 T,6,0 M,3,1 Ng,3,0 E,6,3 S3,3,2 G,6,0 S3,3,3 M,3,2 R,6,3 S2,4,3 Ng,3,1 M,3,3 S1,7,0 T,6,2 J,4,0 Ng,3,2 J,4,1 S1,7,1 G,6,2 S1,7,2 J,4,2 S1,7,3 Ng,3,3 S2,5,0 Qy,6 J,4,3 E,7,0 S2,5,1 Qz,4 R,7,0 S2,5,2 E,7,1 E,7,2 R,7,1 S3,4,0 M,4,0 S3,4,1 R,7,2 T,7,0 M,4,1 Ng,4,0 E,7,3 S3,4,2 G,7,0 S3,4,3 M,4,2 R,7,3 S2,5,3 Ng,4,1 M,4,3 T,7,2 J,5,0 Ng,4,2 G,7,2 J,5,1 Qy,7 J,5,2 Ng,4,3 S2,6,0 J,5,3 S2,6,1 J,6,0 S2,6,2 Qz,5 S2,6,3 J,6,1 S3,5,0 J,6,2 S3,5,1 S3,5,2 M,5,0 S3,5,3 S2,7,0 M,5,1 Ng,5,0 S2,7,1 M,5,2 M,5,3 S2,7,2 Ng,5,1 J,6,3 S2,7,3 J,7,0 Ng,5,2 Qz,6 J,7,1 Ng,5,3 S3,6,0 S3,6,1 J,7,2 S3,6,2 S3,6,3 M,6,0 M,6,1 Ng,6,0 M,6,2 M,6,3 Ng,6,1 Nv,6,2 J,7,3 Ng,6,3 Qz,7 S3,7,0 S3,7,1 M,7,0 S3,7,2 S3,7,3 M,7,1 M,7,2 Ng,7,1 M,7,3 Nv,7,0 Ng,7,3 Nv,7,2"""
 COPY = mybir.ActivationFunctionType.Copy
-INTER = "bbvsssss"
-E_OFF = ()
-J_OFF = ()
-V_ADD = ((7,0),(7,2),(6,2))
 
 
 def tile_orchestra_bleed_mix_t2_kernel(
@@ -66,11 +63,11 @@ def tile_orchestra_bleed_mix_t2_kernel(
         def load_x(r, f0, f1):
             nc.sync.dma_start(out=raws[r][:, :, f0:f1], in_=x.rearrange("(p j) r f -> p j r f", j=4)[:, :, r, f0:f1])
 
-        nc.sync.dma_start(out=words(a_raw[:]), in_=words(a_words[0]))
-        for q in range(4):
-            nc.sync.dma_start(out=words(a_sraw[32 * q : 32 * q + 4, :]), in_=words(a_scales[0, 4 * q : 4 * q + 4, :]))
-        nc.sync.dma_start(out=damp_t[:], in_=damp.rearrange("(p t) -> p t", t=4))
         load_x(0, 0, W)
+        nc.scalar.dma_start(out=words(a_raw[:]), in_=words(a_words[0]))
+        for q in range(4):
+            nc.scalar.dma_start(out=words(a_sraw[32 * q : 32 * q + 4, :]), in_=words(a_scales[0, 4 * q : 4 * q + 4, :]))
+        nc.scalar.dma_start(out=damp_t[:], in_=damp.rearrange("(p t) -> p t", t=4))
         load_x(0, W, F)
         load_x(1, 0, F)
         nc.sync.dma_start(out=words(l_cod[:]), in_=words(l_words.rearrange("g p n -> p g n")))
@@ -92,11 +89,17 @@ def tile_orchestra_bleed_mix_t2_kernel(
 
         damp_f = keep.tile([P, 4], F32)
 
-        nc.vector.tensor_copy(out=a_cod[:].rearrange("p (t m b) -> p t m b", t=4, b=2), in_=a_raw[:].rearrange("p (m t b) -> p t m b", t=4, b=2))
-        nc.vector.tensor_copy(out=a_sc[:], in_=a_sraw[:].rearrange("p (m t) -> p t m", t=4))
+        def order_a():
+            nc.vector.tensor_copy(
+                out=a_cod[:].rearrange("p (t m b) -> p t m b", t=4, b=2),
+                in_=a_raw[:].rearrange("p (m t b) -> p t m b", t=4, b=2),
+            )
+            nc.vector.tensor_copy(out=a_sc[:], in_=a_sraw[:].rearrange("p (m t) -> p t m", t=4))
+            nc.vector.tensor_copy(out=damp_f[:], in_=damp_t[:])
 
         xg, xc, xs = {}, {}, {}
-        y, yt, yc, ys = {}, {}, {}, {}
+        et, jt, res = {}, {}, {}
+        y, yb, yt, yc, ys = {}, {}, {}, {}, {}
         z, zc, zs = {}, {}, {}
         acc, tr = {}, {}
 
@@ -136,47 +139,60 @@ def tile_orchestra_bleed_mix_t2_kernel(
         def bleed(u, t):
             r, g = divmod(u, 2)
             if r not in y:
-                y[r] = work.tile([P, 4, 2, 4, P], F32, align_bytes=64, name="y")
-            if (u, t) in E_OFF:
-                et = work.tile([P, 4, P], F32, name="et", bufs=2)
-                nc.scalar.activation(
-                    out=et[:], in_=acc["E", u, t][:].rearrange("p (m s) -> p s m", s=4), func=COPY, scale=damp_f[:, t : t + 1]
-                )
-                nc.gpsimd.tensor_tensor(
-                    out=y[r][:, t, g, :, :],
-                    in0=et[:],
-                    in1=raws[r][:, t, g * W : (g + 1) * W].rearrange("p (m s) -> p s m", s=4),
-                    op=ADD,
-                )
-                return
+                y[r] = work.tile([P, 4, F], F32, align_bytes=64, name="y")
+            fs = slice(g * W, (g + 1) * W)
             nc.vector.scalar_tensor_tensor(
-                out=y[r][:, t, g, :, :],
-                in0=acc["E", u, t][:].rearrange("p (m s) -> p s m", s=4),
+                out=y[r][:, t, fs],
+                in0=acc["E", u, t][:],
                 scalar=damp_t[:, t : t + 1],
-                in1=raws[r][:, t, g * W : (g + 1) * W].rearrange("p (m s) -> p s m", s=4),
+                in1=raws[r][:, t, fs],
                 op0=MULT,
                 op1=ADD,
             )
 
-        def turn(u, t):
+        def bleed_s(u, t):
+            et[u, t] = work.tile([P, W], F32, name="et", bufs=2)
+            nc.scalar.activation(out=et[u, t][:], in_=acc["E", u, t][:], func=COPY, scale=damp_f[:, t : t + 1])
+
+        def bleed_g(u, t):
             r, g = divmod(u, 2)
-            bank = psum.tile([P, 4, P], F32, name="tr", bufs=TR_BUFS)
-            for s in range(4):
-                nc.tensor.transpose(bank[:, s, :], y[r][:, t, g, s, :], ident[:])
+            fs = slice(g * W, (g + 1) * W)
+            if r not in y:
+                y[r] = work.tile([P, 4, F], F32, align_bytes=64, name="y")
+            nc.gpsimd.tensor_tensor(out=y[r][:, t, fs], in0=et[u, t][:], in1=raws[r][:, t, fs], op=ADD)
+
+        def round_y(u, t):
+            r, g = divmod(u, 2)
+            if u not in yb:
+                yb[u] = work.tile([P, 4, W], BF16, align_bytes=64, name="yb", bufs=2)
+            nc.scalar.copy(out=yb[u][:, t, :], in_=y[r][:, t, g * W : (g + 1) * W])
+
+        def turn1(u, t):
+            bank = tr[u, t] = psum.tile([P, 2, 2, P], F32, name="tr", bufs=TR_BUFS)
+            for tt in range(2):
+                pairs = yb[u][:, t + tt, :].bitcast(F32)
+                for h in range(2):
+                    nc.tensor.transpose(bank[:, tt, h, :], pairs[:, h:256:2], ident[:])
+
+        def turn2(u, t):
             if u not in yt:
-                yt[u] = work.tile([P, 512, 4], BF16, align_bytes=64, name="yt")
-            nc.scalar.copy(out=yt[u][:, t * P : (t + 1) * P, :], in_=bank[:].rearrange("p s j -> p j s"))
+                yt[u] = work.tile([P, 4 * 512], BF16, align_bytes=64, name="yt", bufs=2)
+            nc.scalar.copy(
+                out=yt[u][:].bitcast(F32).rearrange("p (t j h) -> p t j h", t=4, h=2)[:, t : t + 2],
+                in_=tr[u, t][:].rearrange("p t h j -> p t j h"),
+            )
 
         def quant_y(u):
             yc[u] = work.tile([P, 512], U32, align_bytes=64, name="yc", bufs=4)
             ys[u] = work.tile([P, 512], U8, align_bytes=64, name="ys", bufs=4)
             nc.vector.quantize_mx(
-                out=yc[u][:].bitcast(E4M3), scales=ys[u][:], in_=yt[u][:].rearrange("p j s -> p (j s)")
+                out=yc[u][:].bitcast(E4M3), scales=ys[u][:], in_=yt[u][:]
             )
 
-        def mm2(r, b):
+        def mm2(v, k):
+            r, b = v // 2, 4 * (v % 2) + k
             bank = psum.tile([P, 4, P], F32, name="acc", bufs=ACC_BUFS)
-            acc["J", r, b] = bank
+            acc["J", v, k] = bank
             for t in range(4):
                 for g in range(2):
                     u = 2 * r + g
@@ -190,34 +206,36 @@ def tile_orchestra_bleed_mix_t2_kernel(
                         stop=(g == 1),
                     )
 
-        def leak(r, b):
-            g, bb = divmod(b, 4)
-            v = 2 * r + g
+        def leak_views(v, k):
+            r, g = divmod(v, 2)
+            b = 4 * g + k
             if v not in z:
-                z[v] = work.tile([P, 4, P, 4], BF16, align_bytes=64, name="z")
-            ms = slice(32 * bb, 32 * bb + 32)
-            if (v, bb) in J_OFF:
-                jt = work.tile([P, 4, P], F32, name="jt", bufs=2)
-                nc.scalar.copy(out=jt[:], in_=acc["J", r, b][:])
-                nc.gpsimd.tensor_tensor(
-                    out=z[v][:, :, ms, :],
-                    in0=jt[:].rearrange("p t (m s) -> p s m t", s=4),
-                    in1=y[r][:, :, g, :, ms].rearrange("p t s m -> p s m t"),
-                    op=ADD,
-                )
-                return
+                z[v] = work.tile([P, W, 4], BF16, align_bytes=64, name="z")
+            z_out = z[v][:, P * k : P * (k + 1), :].rearrange("p (c i) t -> p c t i", i=2)
+            y_in = y[r][:, :, P * b : P * (b + 1)].rearrange("p t (c i) -> p c t i", i=2)
+            return z_out, y_in
+
+        def leak(v, k):
+            z_out, y_in = leak_views(v, k)
             nc.vector.tensor_tensor(
-                out=z[v][:, :, ms, :],
-                in0=acc["J", r, b][:].rearrange("p t (m s) -> p s m t", s=4),
-                in1=y[r][:, :, g, :, ms].rearrange("p t s m -> p s m t"),
-                op=ADD,
+                out=z_out, in0=acc["J", v, k][:].rearrange("p t (c i) -> p c t i", i=2), in1=y_in, op=ADD
+            )
+
+        def leak_s(v, k):
+            jt[v, k] = work.tile([P, 4, P], F32, name="jt", bufs=2)
+            nc.scalar.copy(out=jt[v, k][:], in_=acc["J", v, k][:])
+
+        def leak_g(v, k):
+            z_out, y_in = leak_views(v, k)
+            nc.gpsimd.tensor_tensor(
+                out=z_out, in0=jt[v, k][:].rearrange("p t (c i) -> p c t i", i=2), in1=y_in, op=ADD
             )
 
         def quant_z(v):
             zc[v] = work.tile([P, W], U32, align_bytes=64, name="zc")
             zs[v] = work.tile([P, W], U8, align_bytes=64, name="zs")
             nc.vector.quantize_mx(
-                out=zc[v][:].bitcast(E4M3), scales=zs[v][:], in_=z[v][:].rearrange("p s m t -> p (s m t)")
+                out=zc[v][:].bitcast(E4M3), scales=zs[v][:], in_=z[v][:].rearrange("p f t -> p (f t)")
             )
 
         def mm3(v, m):
@@ -234,75 +252,28 @@ def tile_orchestra_bleed_mix_t2_kernel(
             )
 
         def mix(v, m):
+            g = v % 2
+            res[v, m] = work.tile([P, W], F32, name="res", bufs=4)
+            nc.vector.tensor_tensor(
+                out=res[v, m][:], in0=acc["M", v, m][:], in1=resp_t[:, g * W : (g + 1) * W], op=MULT
+            )
+
+        def record(v, m, engine):
             r, g = divmod(v, 2)
             fs = slice(g * W, (g + 1) * W)
-            res = work.tile([P, W], F32, name="res", bufs=4)
-            nc.vector.tensor_tensor(
-                out=res[:].rearrange("p (m s) -> p m s", s=4),
-                in0=acc["M", v, m][:].rearrange("p (s m) -> p m s", s=4),
-                in1=resp_t[:, fs].rearrange("p (m s) -> p m s", s=4),
-                op=MULT,
-            )
             fin = work.tile([P, W], F32, name="fin", bufs=6)
-            add_engine = nc.vector if (v, m) in V_ADD else nc.gpsimd
-            add_engine.tensor_tensor(out=fin[:], in0=res[:], in1=rec_t[:, m, r, fs], op=ADD)
+            engine.tensor_tensor(out=fin[:], in0=res[v, m][:], in1=rec_t[:, m, r, fs], op=ADD)
             nc.sync.dma_start(out=out[m * P : (m + 1) * P, r, fs], in_=fin[:])
 
-        order = [("Qx", 0)]
-        late = []
-        for h in range(11):
-            e = [("E", h, t) for t in range(4)] if h < 8 else []
-            m = [("M", h - 3, k) for k in range(4)] if 0 <= h - 3 < 8 else []
-            j = [("J",) + ((h - 2) // 2, 4 * ((h - 2) % 2) + k) for k in range(4)] if 0 <= h - 2 < 8 else []
-            qz = [("Qz", h - 3)] if 0 <= h - 3 < 8 else []
-            qy = [("Qy", h - 1)] if 0 <= h - 1 < 8 else []
-            if h < 8:
-                order += e[0:1] + qz + e[1:2] + qy + e[2:3] + m[0:2] + e[3:4] + m[2:4]
-                if h < 7:
-                    order += [("Qx", h + 1)]
-                order += j
-            elif h == 8:
-                order += qz + m[0:2] + qy + m[2:4] + j[0:4]
-            elif h == 9:
-                order += j[0:1] + qz + j[1:4] + m[0:2]
-                late = m[2:4]
-            else:
-                order += qz + late + m
-
-        banks = [i for i in range(len(order)) if order[i][0] in ("E", "J", "M")]
-        make = {"E": mm1, "J": mm2, "M": mm3}
-        use = {"E": bleed, "J": leak, "M": mix, "Qx": quant_x, "Qy": quant_y, "Qz": quant_z}
-        feeds = {"E": lambda k: ("Qx", k[1]), "J": lambda k: ("Qy", 2 * k[1] + 1), "M": lambda k: ("Qz", k[1])}
-
-        def inter(u):
-            if u < T * 2:
-                if INTER[u] == "b":
-                    interleave(u, "s", 256, 512)
-                    interleave(u, "v", 0, 256)
-                else:
-                    interleave(u, INTER[u], 0, W)
-
-        inter(0)
-        nc.vector.tensor_copy(out=damp_f[:], in_=damp_t[:])
-        done = set()
-        filled = 0
-        turns = []
-        for i in range(len(order)):
-            op = order[i]
-            ahead = len([b for b in banks if b < i]) + ACC_BUFS
-            while filled < min(ahead, len(banks)):
-                nxt = order[banks[filled]]
-                if feeds[nxt[0]](nxt) not in done:
-                    break
-                make[nxt[0]](*nxt[1:])
-                filled += 1
-            use[op[0]](*op[1:])
-            done.add(op)
-            if op[0] == "Qx":
-                inter(op[1] + 1)
-            if op[0] == "E":
-                turns.append(op[1:])
-            if len(turns) >= 2 and op[0] != "E" or len(turns) == 3:
-                for w in turns[:2]:
-                    turn(*w)
-                turns = turns[2:]
+        do = {
+            "Iv": lambda u, a, b: interleave(u, "v", a, b),
+            "Is": lambda u, a, b: interleave(u, "s", a, b),
+            "Ig": lambda u, a, b: interleave(u, "g", a, b),
+            "Qx": quant_x, "S1": mm1, "E": bleed, "Es": bleed_s, "Eg": bleed_g, "R": round_y, "T": turn1, "G": turn2,
+            "Qy": quant_y, "S2": mm2, "J": leak, "Js": leak_s, "Jg": leak_g, "Qz": quant_z, "S3": mm3, "M": mix,
+            "Nv": lambda v, m: record(v, m, nc.vector), "Ng": lambda v, m: record(v, m, nc.gpsimd),
+            "A": order_a,
+        }
+        for op in PROG.split():
+            parts = op.split(",")
+            do[parts[0]](*[int(q) for q in parts[1:]])

@@ -20,7 +20,7 @@ FLOPS = 2 * (2 * S * S * T * F + S * T * F * F)
 
 ACC_BUFS = 6
 TR_BUFS = 2
-PROG = """A Is,0,256,512 Iv,0,0,256 Iv,1,0,256 Is,1,256,512 Qx,0 Iv,2,0,512 S1,0,0 S1,0,1 S1,0,2 S1,0,3 E,0,0 Qx,1 R,0,0 E,0,1 S1,1,0 S1,1,1 E,0,2 R,0,1 S1,1,2 S1,1,3 E,0,3 R,0,2 T,0,0 E,1,0 R,0,3 Qx,2 G,0,0 T,0,2 E,1,1 R,1,0 S1,2,0 S1,2,1 E,1,2 G,0,2 S1,2,2 S1,2,3 E,1,3 R,1,1 Qy,0 R,1,2 T,1,0 Iv,3,0,512 R,1,3 G,1,0 T,1,2 Is,4,0,128 E,2,0 G,1,2 Qx,3 R,2,0 Qy,1 S1,3,0 Is,4,128,256 S1,3,1 E,2,1 S2,0,0 Is,4,256,384 E,2,2 S2,0,1 E,2,3 R,2,1 S2,0,2 J,0,0 R,2,2 S2,0,3 J,0,1 R,2,3 S1,3,2 J,0,2 Is,4,384,512 S1,3,3 J,0,3 T,2,0 Is,5,0,128 E,3,0 T,2,2 G,2,0 Qz,0 S2,1,0 G,2,2 Qx,4 S2,1,1 R,3,0 Qy,2 Is,5,128,256 S3,0,0 E,3,1 Is,5,256,384 M,0,0 S3,0,1 R,3,1 M,0,1 S3,0,2 Ng,0,0 Is,5,384,512 T,3,0 M,0,2 Is,6,0,128 E,3,2 S3,0,3 Ng,0,1 S2,1,2 M,0,3 G,3,0 S2,1,3 E,3,3 R,3,2 Ng,0,2 S1,4,0 J,1,0 Is,6,128,256 S1,4,1 J,1,1 S1,4,2 R,3,3 Ng,0,3 J,1,2 S1,4,3 Is,6,256,384 T,3,2 J,1,3 Is,6,384,512 E,4,0 G,3,2 Qz,1 R,4,0 Qy,3 S3,1,0 Is,7,0,128 S3,1,1 Qx,5 S3,1,2 Is,7,128,256 M,1,0 Is,7,256,384 M,1,1 S3,1,3 Ng,1,0 Is,7,384,512 M,1,2 S2,2,0 M,1,3 Ng,1,1 S2,2,1 E,4,1 S2,2,2 E,4,2 R,4,1 Ng,1,2 S2,2,3 E,4,3 R,4,2 S1,5,0 J,2,0 S1,5,1 R,4,3 Ng,1,3 T,4,0 J,2,1 T,4,2 J,2,2 G,4,0 J,2,3 S1,5,2 G,4,2 S1,5,3 E,5,0 S2,3,0 Qy,4 S2,3,1 R,5,0 Qz,2 S2,3,2 Qx,6 E,5,1 E,5,2 R,5,1 S3,2,0 M,2,0 S3,2,1 R,5,2 T,5,0 M,2,1 Ng,2,0 E,5,3 S3,2,2 G,5,0 S3,2,3 M,2,2 R,5,3 S2,3,3 Ng,2,1 M,2,3 S1,6,0 T,5,2 J,3,0 Ng,2,2 J,3,1 S1,6,1 G,5,2 S1,6,2 J,3,2 S1,6,3 Ng,2,3 Qy,5 J,3,3 S2,4,0 E,6,0 S2,4,1 Qz,3 R,6,0 S2,4,2 Qx,7 E,6,1 E,6,2 R,6,1 S3,3,0 M,3,0 S3,3,1 R,6,2 T,6,0 M,3,1 Ng,3,0 E,6,3 S3,3,2 G,6,0 S3,3,3 M,3,2 R,6,3 S2,4,3 Ng,3,1 M,3,3 S1,7,0 T,6,2 J,4,0 Ng,3,2 J,4,1 S1,7,1 G,6,2 S1,7,2 J,4,2 S1,7,3 Ng,3,3 S2,5,0 Qy,6 J,4,3 E,7,0 S2,5,1 Qz,4 R,7,0 S2,5,2 E,7,1 E,7,2 R,7,1 S3,4,0 M,4,0 S3,4,1 R,7,2 T,7,0 M,4,1 Ng,4,0 E,7,3 S3,4,2 G,7,0 S3,4,3 M,4,2 R,7,3 S2,5,3 Ng,4,1 M,4,3 T,7,2 J,5,0 Ng,4,2 G,7,2 J,5,1 Qy,7 J,5,2 Ng,4,3 S2,6,0 J,5,3 S2,6,1 J,6,0 S2,6,2 Qz,5 S2,6,3 J,6,1 S3,5,0 J,6,2 S3,5,1 S3,5,2 M,5,0 S3,5,3 S2,7,0 M,5,1 Ng,5,0 S2,7,1 M,5,2 M,5,3 S2,7,2 Ng,5,1 J,6,3 S2,7,3 J,7,0 Ng,5,2 Qz,6 J,7,1 Ng,5,3 S3,6,0 S3,6,1 J,7,2 S3,6,2 S3,6,3 M,6,0 M,6,1 Ng,6,0 M,6,2 M,6,3 Ng,6,1 Nv,6,2 J,7,3 Ng,6,3 Qz,7 S3,7,0 S3,7,1 M,7,0 S3,7,2 S3,7,3 M,7,1 M,7,2 Ng,7,1 M,7,3 Nv,7,0 Ng,7,3 Nv,7,2"""
+PROG = """A Iv,0,0,512 Is,1,256,512 Iv,1,0,256 Is,2,256,512 Qx,0 Qx,1 S1,0,0 S1,0,1 E,0,0 S1,0,2 S1,0,3 E,0,1 S1,1,0 Rg,0,0 Es,0,3 S1,1,1 S1,1,2 E,0,2 Rg,0,1 S1,1,3 Is,4,0,128 E,1,0 Rg,0,2 T,0,0 Es,1,3 E,1,1 Rg,1,0 G,0,0 E,1,2 Rg,1,1 Is,4,128,256 Iv,2,0,256 Rg,1,2 T,1,0 Is,4,256,384 Iv,3,0,512 Eg,0,3 G,1,0 Is,4,384,512 Qx,2 Eg,1,3 Is,5,0,128 Qx,3 S1,2,0 S1,2,1 Is,5,128,256 Rg,0,3 E,2,0 S1,2,2 S1,2,3 Is,5,256,384 E,2,1 Rg,1,3 S1,3,0 S1,3,1 S1,3,2 E,2,2 Rg,2,0 Es,2,3 S1,3,3 E,3,0 T,0,2 Es,3,3 Rg,2,1 T,1,2 E,3,1 G,0,2 Rg,2,2 E,3,2 G,1,2 T,2,0 Rg,3,0 Is,5,384,512 C Qy,0 Rg,3,1 G,2,0 Qy,1 Rg,3,2 T,3,0 Is,6,128,256 Qx,4 Eg,2,3 S2,0,0 G,3,0 Qx,5 S2,0,1 Js,0,0 Iv,6,0,128 Eg,3,3 S2,0,2 J,0,1 Is,6,256,384 S2,0,3 J,0,2 Is,6,384,512 Rg,2,3 S1,4,0 J,0,3 S1,4,1 Rg,3,3 Is,7,0,128 S1,4,2 S1,4,3 E,4,0 S2,1,0 Jg,0,0 Is,7,128,256 E,4,1 S2,1,1 Es,4,3 E,4,2 Rg,4,0 S2,1,2 Js,1,0 S2,1,3 Qz,0 Is,7,256,384 S1,5,0 J,1,1 Rg,4,1 Is,7,384,512 S1,5,1 S1,5,2 J,1,2 Rg,4,2 S1,5,3 T,2,2 Es,5,3 J,1,3 Eg,4,3 T,3,2 E,5,0 G,2,2 P3,0,0 E,5,1 G,3,2 Rg,5,0 P3,0,1 P3,0,2 Rs,4,3 P3,0,3 Qy,2 Rg,5,1 T,4,0 Ps,0,0 Qy,3 T,4,2 G,4,0 E,5,2 Jg,1,0 S2,2,0 G,4,2 S2,2,1 Js,2,0 Qx,6 Rg,5,2 S2,2,2 Js,2,1 Qz,1 S2,2,3 Ps,0,1 J,2,2 Eg,5,3 S1,6,0 Ps,0,2 S1,6,1 J,2,3 S1,6,2 Ps,0,3 S1,6,3 Jg,2,0 E,6,0 S2,3,0 Es,6,3 E,6,1 S2,3,1 Js,3,0 Rg,5,3 E,6,2 S2,3,2 Js,3,1 Rg,6,0 S2,3,3 Qx,7 P3,1,0 P3,1,1 Ps,1,0 J,3,2 Rg,6,1 P3,1,2 P3,1,3 Ps,1,1 J,3,3 Rg,6,2 S1,7,0 S1,7,1 E,7,0 Ps,1,2 S1,7,2 Jg,2,1 S1,7,3 E,7,2 Ps,1,3 Pt,0,0 Pt,0,1 M,0,0 Es,7,1 Rg,7,0 Pt,0,2 Pt,0,3 M,0,1 Es,7,3 Rg,7,2 T,5,0 M,0,2 T,5,2 Eg,6,3 G,5,0 M,0,3 Pt,1,0 G,5,2 Pt,1,1 Pt,1,2 Qz,2 Jg,3,0 Rs,6,3 Pt,1,3 T,6,0 Qy,5,1 T,6,2 G,6,0 P3,2,0 M,1,0 Jg,3,1 G,6,2 P3,2,1 Ps,2,0 M,1,1 S2,4,0 Eg,7,1 M,1,2 Ps,2,1 S2,4,1 M,1,3 Js,4,0 S2,4,2 Eg,7,3 Rs,7,1 S2,4,3 Js,4,1 P3,2,2 P3,2,3 Qz,3 S2,5,0 Rs,7,3 J,4,2 Jg,4,0 S2,5,1 Ps,2,2 J,4,3 S2,5,2 Ps,2,3 Jg,4,1 S2,5,3 Js,5,0 J,5,2 P3,3,0 Js,5,1 J,5,3 P3,3,1 Jg,5,0 P3,3,2 Ps,3,0 P3,3,3 Pt,2,0 Ps,3,1 Pt,2,1 Qz,4 Pt,2,2 Ps,3,2 Pt,2,3 M,2,0 Jg,5,1 T,7,0 Ps,3,3 M,2,1 T,7,2 G,7,0 M,2,2 Pt,3,0 G,7,2 Pt,3,1 M,2,3 Pt,3,2 Pt,3,3 Qy,7,1 P3,4,0 P3,4,1 Ps,4,0 M,3,0 Ps,4,1 P3,4,2 M,3,1 S2,6,0 Ps,4,2 M,3,2 S2,6,1 Js,6,0 M,3,3 S2,6,2 Js,6,1 Jg,6,0 S2,6,3 Js,6,2 P3,4,3 Qz,5 S2,7,0 Ps,4,3 J,6,3 Jg,6,1 S2,7,1 J,7,0 S2,7,2 Jg,6,2 J,7,1 S2,7,3 J,7,2 P3,5,0 P3,5,1 Ps,5,0 P3,5,2 Qz,6 P3,5,3 Ps,5,1 J,7,3 Pt,4,0 Pt,4,1 Ps,5,2 M,4,0 Pt,4,2 Pt,4,3 Ps,5,3 M,4,1 P3,6,0 P3,6,1 M,4,2 Ps,6,0 P3,6,2 P3,6,3 M,4,3 Ps,6,1 Pt,5,0 Pt,5,1 Qz,7 Ps,6,2 Pt,5,2 Pt,5,3 M,5,0 Ps,6,3 P3,7,0 M,5,1 P3,7,1 Ps,7,0 P3,7,2 M,5,2 P3,7,3 Ps,7,1 Pt,6,0 M,5,3 Pt,6,1 Ps,7,2 Pt,6,2 M,6,0 Pt,6,3 Ps,7,3 M,6,1 Pt,7,0 M,6,2 Pt,7,1 Pt,7,2 M,6,3 Pt,7,3 M,7,0 M,7,1 M,7,2 M,7,3"""
 COPY = mybir.ActivationFunctionType.Copy
 
 
@@ -43,8 +43,9 @@ def tile_orchestra_bleed_mix_t2_kernel(
         m_cod = keep.tile([P, 2 * C], U8, align_bytes=64)
         m_sc = keep.tile([P, C], U8, align_bytes=64)
         damp_t = keep.tile([P, 4], BF16)
-        resp_t = keep.tile([P, F], BF16, align_bytes=64)
-        rec_t = keep.tile([P, 4, T, F], BF16, align_bytes=64)
+        resp_row = keep.tile([P, P], BF16, align_bytes=64)
+        resp_c = keep.tile([P, 8], F32)
+        ident_b = keep.tile([P, P], BF16, align_bytes=64)
         ident = keep.tile([P, P], F32, align_bytes=64)
 
         def words(tile):
@@ -53,7 +54,9 @@ def tile_orchestra_bleed_mix_t2_kernel(
         nc.vector.memset(words(a_sraw[:]), 0)
         nc.vector.memset(words(l_sc[:]), 0)
         nc.vector.memset(words(m_sc[:]), 0)
+        nc.gpsimd.memset(resp_row[:], 0.0)
         make_identity(nc, ident[:])
+        make_identity(nc, ident_b[:])
 
         raws = []
         for r in range(T):
@@ -80,12 +83,16 @@ def tile_orchestra_bleed_mix_t2_kernel(
         nc.sync.dma_start(out=words(m_cod[:]), in_=words(m_words[0]))
         for q in range(4):
             nc.sync.dma_start(out=words(m_sc[32 * q : 32 * q + 4, :]), in_=words(m_scales[0, 4 * q : 4 * q + 4, :]))
-        nc.sync.dma_start(out=resp_t[:], in_=resp.partition_broadcast(P))
-        rec_v = rec.rearrange("(m c) r f -> c m r f", c=P)
-        nc.sync.dma_start(out=rec_t[:, :, 0, :], in_=rec_v[:, :, 0, :])
+        nc.sync.dma_start(out=resp_row[0:8, :], in_=resp.rearrange("(b q) -> b q", q=P))
         load_x(3, 0, F)
-        for r in range(1, T):
-            nc.sync.dma_start(out=rec_t[:, :, r, :], in_=rec_v[:, :, r, :])
+        recs = {}
+
+        def load_rec(r):
+            recs[r] = work.tile([P, 4, F], BF16, align_bytes=64, name="rec", bufs=3)
+            nc.sync.dma_start(out=recs[r][:], in_=rec.rearrange("(m c) r f -> c m r f", c=P)[:, :, r, :])
+
+        for r in range(3):
+            load_rec(r)
 
         damp_f = keep.tile([P, 4], F32)
 
@@ -105,9 +112,9 @@ def tile_orchestra_bleed_mix_t2_kernel(
 
         def interleave(u, engine, c0, c1):
             r, g = divmod(u, 2)
-            if u not in xg:
-                xg[u] = work.tile([P, W, 4], BF16, align_bytes=64, name="xg")
-            o = xg[u][:, c0:c1, :].rearrange("p (c i) t -> p c t i", i=4)
+            if r not in xg:
+                xg[r] = work.tile([P, 2, W, 4], BF16, align_bytes=64, name="xg", bufs=2)
+            o = xg[r][:, g, c0:c1, :].rearrange("p (c i) t -> p c t i", i=4)
             i_ = raws[r][:, :, g * W + c0 : g * W + c1].rearrange("p t (c i) -> p c t i", i=4)
             if engine == "v":
                 nc.vector.tensor_copy(out=o, in_=i_)
@@ -116,11 +123,17 @@ def tile_orchestra_bleed_mix_t2_kernel(
             else:
                 nc.scalar.copy(out=o, in_=i_)
 
-        def quant_x(u):
-            xc[u] = work.tile([P, W], U32, align_bytes=64, name="xc")
-            xs[u] = work.tile([P, W], U8, align_bytes=64, name="xs")
+        def quant_x(u, whole=0):
+            r, g = divmod(u, 2)
+            gs = slice(0, 2) if whole else slice(g, g + 1)
+            if r not in xc:
+                xc[r] = work.tile([P, 2 * W], U32, align_bytes=64, name="xc", bufs=2)
+                xs[r] = work.tile([P, 2 * W], U8, align_bytes=64, name="xs", bufs=2)
+            cs = slice(gs.start * W, gs.stop * W)
             nc.vector.quantize_mx(
-                out=xc[u][:].bitcast(E4M3), scales=xs[u][:], in_=xg[u][:].rearrange("p w t -> p (w t)")
+                out=xc[r][:, cs].bitcast(E4M3),
+                scales=xs[r][:, cs],
+                in_=xg[r][:, gs].rearrange("p g w t -> p (g w t)"),
             )
 
         def mm1(u, t):
@@ -130,8 +143,8 @@ def tile_orchestra_bleed_mix_t2_kernel(
                 out=bank[:],
                 lhsT=a_cod[:, 2 * P * t : 2 * P * (t + 1)].bitcast(E2M1),
                 lhsT_scale=a_sc[:, t, :],
-                rhs=xc[u][:].bitcast(E4M3),
-                rhs_scale=xs[u][:],
+                rhs=xc[u // 2][:, W * (u % 2) : W * (u % 2 + 1)].bitcast(E4M3),
+                rhs_scale=xs[u // 2][:, W * (u % 2) : W * (u % 2 + 1)],
                 start=True,
                 stop=True,
             )
@@ -161,11 +174,15 @@ def tile_orchestra_bleed_mix_t2_kernel(
                 y[r] = work.tile([P, 4, F], F32, align_bytes=64, name="y")
             nc.gpsimd.tensor_tensor(out=y[r][:, t, fs], in0=et[u, t][:], in1=raws[r][:, t, fs], op=ADD)
 
-        def round_y(u, t):
+        def round_y(u, t, engine):
             r, g = divmod(u, 2)
             if u not in yb:
                 yb[u] = work.tile([P, 4, W], BF16, align_bytes=64, name="yb", bufs=2)
-            nc.scalar.copy(out=yb[u][:, t, :], in_=y[r][:, t, g * W : (g + 1) * W])
+            y_in = y[r][:, t, g * W : (g + 1) * W]
+            if engine == "s":
+                nc.scalar.copy(out=yb[u][:, t, :], in_=y_in)
+            else:
+                nc.gpsimd.tensor_scalar(out=yb[u][:, t, :], in0=y_in, scalar1=1.0, scalar2=0.0, op0=MULT, op1=ADD)
 
         def turn1(u, t):
             bank = tr[u, t] = psum.tile([P, 2, 2, P], F32, name="tr", bufs=TR_BUFS)
@@ -175,19 +192,29 @@ def tile_orchestra_bleed_mix_t2_kernel(
                     nc.tensor.transpose(bank[:, tt, h, :], pairs[:, h:256:2], ident[:])
 
         def turn2(u, t):
-            if u not in yt:
-                yt[u] = work.tile([P, 4 * 512], BF16, align_bytes=64, name="yt", bufs=2)
+            r, g = divmod(u, 2)
+            if r not in yt:
+                yt[r] = work.tile([P, 2 * 4 * 512], BF16, align_bytes=64, name="yt", bufs=2)
             nc.scalar.copy(
-                out=yt[u][:].bitcast(F32).rearrange("p (t j h) -> p t j h", t=4, h=2)[:, t : t + 2],
+                out=yt[r][:].bitcast(F32).rearrange("p (g t j h) -> p g t j h", g=2, t=4, h=2)[:, g, t : t + 2],
                 in_=tr[u, t][:].rearrange("p t h j -> p t j h"),
             )
 
-        def quant_y(u):
-            yc[u] = work.tile([P, 512], U32, align_bytes=64, name="yc", bufs=4)
-            ys[u] = work.tile([P, 512], U8, align_bytes=64, name="ys", bufs=4)
-            nc.vector.quantize_mx(
-                out=yc[u][:].bitcast(E4M3), scales=ys[u][:], in_=yt[u][:]
-            )
+        def quant_y(u, whole=0):
+            r, g = divmod(u, 2)
+            if r not in yc:
+                yc[r] = work.tile([P, 2, 512], U32, align_bytes=64, name="yc", bufs=2)
+                ys[r] = work.tile([P, 2, 512], U8, align_bytes=64, name="ys", bufs=2)
+            if whole:
+                nc.vector.quantize_mx(
+                    out=yc[r][:].rearrange("p g j -> p (g j)").bitcast(E4M3),
+                    scales=ys[r][:].rearrange("p g j -> p (g j)"),
+                    in_=yt[r][:],
+                )
+            else:
+                nc.vector.quantize_mx(
+                    out=yc[r][:, g, :].bitcast(E4M3), scales=ys[r][:, g, :], in_=yt[r][:, 2048 * g : 2048 * (g + 1)]
+                )
 
         def mm2(v, k):
             r, b = v // 2, 4 * (v % 2) + k
@@ -195,11 +222,10 @@ def tile_orchestra_bleed_mix_t2_kernel(
             acc["J", v, k] = bank
             for t in range(4):
                 for g in range(2):
-                    u = 2 * r + g
                     nc.tensor.matmul_mx(
                         out=bank[:, t, :],
-                        lhsT=yc[u][:, t * P : (t + 1) * P].bitcast(E4M3),
-                        lhsT_scale=ys[u][:, t * P : (t + 1) * P],
+                        lhsT=yc[r][:, g, t * P : (t + 1) * P].bitcast(E4M3),
+                        lhsT_scale=ys[r][:, g, t * P : (t + 1) * P],
                         rhs=l_cod[:, g, 2 * P * b : 2 * P * (b + 1)].bitcast(E2M1),
                         rhs_scale=l_sc[:, g, P * b : P * (b + 1)],
                         start=(g == 0),
@@ -238,41 +264,55 @@ def tile_orchestra_bleed_mix_t2_kernel(
                 out=zc[v][:].bitcast(E4M3), scales=zs[v][:], in_=z[v][:].rearrange("p f t -> p (f t)")
             )
 
-        def mm3(v, m):
-            bank = psum.tile([P, W], F32, name="acc", bufs=ACC_BUFS)
-            acc["M", v, m] = bank
+        def columns_of_resp():
+            bank = psum.tile([P, P], BF16, name="tr", bufs=TR_BUFS)
+            nc.tensor.transpose(bank[:], resp_row[:], ident_b[:])
+            nc.vector.tensor_copy(out=resp_c[:], in_=bank[:, 0:8])
+
+        def mm3(v, k):
+            bank = psum.tile([P, C], F32, name="acc", bufs=ACC_BUFS)
+            acc["P", v, k] = bank
             nc.tensor.matmul_mx(
                 out=bank[:],
-                lhsT=m_cod[:, 2 * P * m : 2 * P * (m + 1)].bitcast(E2M1),
-                lhsT_scale=m_sc[:, P * m : P * (m + 1)],
-                rhs=zc[v][:].bitcast(E4M3),
-                rhs_scale=zs[v][:],
+                lhsT=zc[v][:, P * k : P * (k + 1)].bitcast(E4M3),
+                lhsT_scale=zs[v][:, P * k : P * (k + 1)],
+                rhs=m_cod[:].bitcast(E2M1),
+                rhs_scale=m_sc[:],
                 start=True,
                 stop=True,
             )
 
-        def mix(v, m):
-            g = v % 2
-            res[v, m] = work.tile([P, W], F32, name="res", bufs=4)
-            nc.vector.tensor_tensor(
-                out=res[v, m][:], in0=acc["M", v, m][:], in1=resp_t[:, g * W : (g + 1) * W], op=MULT
-            )
+        def respond(v, k):
+            if v not in res:
+                res[v] = work.tile([P, 4, C], F32, align_bytes=64, name="res", bufs=2)
+            b = 4 * (v % 2) + k
+            nc.scalar.activation(out=res[v][:, k, :], in_=acc["P", v, k][:], func=COPY, scale=resp_c[:, b : b + 1])
 
-        def record(v, m, engine):
+        def back(v, m):
+            bank = psum.tile([P, 4, P], F32, name="acc", bufs=ACC_BUFS)
+            acc["M", v, m] = bank
+            for k in range(4):
+                nc.tensor.transpose(bank[:, k, :], res[v][:, k, P * m : P * (m + 1)], ident[:])
+
+        def record(v, m):
             r, g = divmod(v, 2)
             fs = slice(g * W, (g + 1) * W)
             fin = work.tile([P, W], F32, name="fin", bufs=6)
-            engine.tensor_tensor(out=fin[:], in0=res[v, m][:], in1=rec_t[:, m, r, fs], op=ADD)
+            nc.vector.tensor_tensor(
+                out=fin[:], in0=acc["M", v, m][:].rearrange("p k f -> p (k f)"), in1=recs[r][:, m, fs], op=ADD
+            )
             nc.sync.dma_start(out=out[m * P : (m + 1) * P, r, fs], in_=fin[:])
+            if (v, m) == (2, 0):
+                load_rec(3)
 
         do = {
             "Iv": lambda u, a, b: interleave(u, "v", a, b),
             "Is": lambda u, a, b: interleave(u, "s", a, b),
             "Ig": lambda u, a, b: interleave(u, "g", a, b),
-            "Qx": quant_x, "S1": mm1, "E": bleed, "Es": bleed_s, "Eg": bleed_g, "R": round_y, "T": turn1, "G": turn2,
-            "Qy": quant_y, "S2": mm2, "J": leak, "Js": leak_s, "Jg": leak_g, "Qz": quant_z, "S3": mm3, "M": mix,
-            "Nv": lambda v, m: record(v, m, nc.vector), "Ng": lambda v, m: record(v, m, nc.gpsimd),
-            "A": order_a,
+            "Qx": quant_x, "S1": mm1, "E": bleed, "Es": bleed_s, "Eg": bleed_g,
+            "Rs": lambda u, t: round_y(u, t, "s"), "Rg": lambda u, t: round_y(u, t, "g"), "T": turn1, "G": turn2,
+            "Qy": quant_y, "S2": mm2, "J": leak, "Js": leak_s, "Jg": leak_g, "Qz": quant_z, "C": columns_of_resp,
+            "P3": mm3, "Ps": respond, "Pt": back, "M": record, "A": order_a,
         }
         for op in PROG.split():
             parts = op.split(",")

@@ -18,9 +18,9 @@ P = 128
 W = 512
 FLOPS = 2 * (2 * S * S * T * F + S * T * F * F)
 
-ACC_BUFS = 6
-TR_BUFS = 2
-PROG = """A Iv,0,0,512 Is,1,256,512 Iv,1,0,256 Is,2,256,512 Qx,0 Qx,1 S1,0,0 S1,0,1 E,0,0 S1,0,2 S1,0,3 E,0,1 S1,1,0 Rg,0,0 Es,0,3 S1,1,1 S1,1,2 E,0,2 Rg,0,1 S1,1,3 Is,4,0,128 E,1,0 Rg,0,2 T,0,0 Es,1,3 E,1,1 Rg,1,0 G,0,0 E,1,2 Rg,1,1 Is,4,128,256 Iv,2,0,256 Rg,1,2 T,1,0 Is,4,256,384 Iv,3,0,512 Eg,0,3 G,1,0 Is,4,384,512 Qx,2 Eg,1,3 Is,5,0,128 Qx,3 S1,2,0 S1,2,1 Is,5,128,256 Rg,0,3 E,2,0 S1,2,2 S1,2,3 Is,5,256,384 E,2,1 Rg,1,3 S1,3,0 S1,3,1 S1,3,2 E,2,2 Rg,2,0 Es,2,3 S1,3,3 E,3,0 T,0,2 Es,3,3 Rg,2,1 T,1,2 E,3,1 G,0,2 Rg,2,2 E,3,2 G,1,2 T,2,0 Rg,3,0 Is,5,384,512 C Qy,0 Rg,3,1 G,2,0 Qy,1 Rg,3,2 T,3,0 Is,6,128,256 Qx,4 Eg,2,3 S2,0,0 G,3,0 Qx,5 S2,0,1 Js,0,0 Iv,6,0,128 Eg,3,3 S2,0,2 J,0,1 Is,6,256,384 S2,0,3 J,0,2 Is,6,384,512 Rg,2,3 S1,4,0 J,0,3 S1,4,1 Rg,3,3 Is,7,0,128 S1,4,2 S1,4,3 E,4,0 S2,1,0 Jg,0,0 Is,7,128,256 E,4,1 S2,1,1 Es,4,3 E,4,2 Rg,4,0 S2,1,2 Js,1,0 S2,1,3 Qz,0 Is,7,256,384 S1,5,0 J,1,1 Rg,4,1 Is,7,384,512 S1,5,1 S1,5,2 J,1,2 Rg,4,2 S1,5,3 T,2,2 Es,5,3 J,1,3 Eg,4,3 T,3,2 E,5,0 G,2,2 P3,0,0 E,5,1 G,3,2 Rg,5,0 P3,0,1 P3,0,2 Rs,4,3 P3,0,3 Qy,2 Rg,5,1 T,4,0 Ps,0,0 Qy,3 T,4,2 G,4,0 E,5,2 Jg,1,0 S2,2,0 G,4,2 S2,2,1 Js,2,0 Qx,6 Rg,5,2 S2,2,2 Js,2,1 Qz,1 S2,2,3 Ps,0,1 J,2,2 Eg,5,3 S1,6,0 Ps,0,2 S1,6,1 J,2,3 S1,6,2 Ps,0,3 S1,6,3 Jg,2,0 E,6,0 S2,3,0 Es,6,3 E,6,1 S2,3,1 Js,3,0 Rg,5,3 E,6,2 S2,3,2 Js,3,1 Rg,6,0 S2,3,3 Qx,7 P3,1,0 P3,1,1 Ps,1,0 J,3,2 Rg,6,1 P3,1,2 P3,1,3 Ps,1,1 J,3,3 Rg,6,2 S1,7,0 S1,7,1 E,7,0 Ps,1,2 S1,7,2 Jg,2,1 S1,7,3 E,7,2 Ps,1,3 Pt,0,0 Pt,0,1 M,0,0 Es,7,1 Rg,7,0 Pt,0,2 Pt,0,3 M,0,1 Es,7,3 Rg,7,2 T,5,0 M,0,2 T,5,2 Eg,6,3 G,5,0 M,0,3 Pt,1,0 G,5,2 Pt,1,1 Pt,1,2 Qz,2 Jg,3,0 Rs,6,3 Pt,1,3 T,6,0 Qy,5,1 T,6,2 G,6,0 P3,2,0 M,1,0 Jg,3,1 G,6,2 P3,2,1 Ps,2,0 M,1,1 S2,4,0 Eg,7,1 M,1,2 Ps,2,1 S2,4,1 M,1,3 Js,4,0 S2,4,2 Eg,7,3 Rs,7,1 S2,4,3 Js,4,1 P3,2,2 P3,2,3 Qz,3 S2,5,0 Rs,7,3 J,4,2 Jg,4,0 S2,5,1 Ps,2,2 J,4,3 S2,5,2 Ps,2,3 Jg,4,1 S2,5,3 Js,5,0 J,5,2 P3,3,0 Js,5,1 J,5,3 P3,3,1 Jg,5,0 P3,3,2 Ps,3,0 P3,3,3 Pt,2,0 Ps,3,1 Pt,2,1 Qz,4 Pt,2,2 Ps,3,2 Pt,2,3 M,2,0 Jg,5,1 T,7,0 Ps,3,3 M,2,1 T,7,2 G,7,0 M,2,2 Pt,3,0 G,7,2 Pt,3,1 M,2,3 Pt,3,2 Pt,3,3 Qy,7,1 P3,4,0 P3,4,1 Ps,4,0 M,3,0 Ps,4,1 P3,4,2 M,3,1 S2,6,0 Ps,4,2 M,3,2 S2,6,1 Js,6,0 M,3,3 S2,6,2 Js,6,1 Jg,6,0 S2,6,3 Js,6,2 P3,4,3 Qz,5 S2,7,0 Ps,4,3 J,6,3 Jg,6,1 S2,7,1 J,7,0 S2,7,2 Jg,6,2 J,7,1 S2,7,3 J,7,2 P3,5,0 P3,5,1 Ps,5,0 P3,5,2 Qz,6 P3,5,3 Ps,5,1 J,7,3 Pt,4,0 Pt,4,1 Ps,5,2 M,4,0 Pt,4,2 Pt,4,3 Ps,5,3 M,4,1 P3,6,0 P3,6,1 M,4,2 Ps,6,0 P3,6,2 P3,6,3 M,4,3 Ps,6,1 Pt,5,0 Pt,5,1 Qz,7 Ps,6,2 Pt,5,2 Pt,5,3 M,5,0 Ps,6,3 P3,7,0 M,5,1 P3,7,1 Ps,7,0 P3,7,2 M,5,2 P3,7,3 Ps,7,1 Pt,6,0 M,5,3 Pt,6,1 Ps,7,2 Pt,6,2 M,6,0 Pt,6,3 Ps,7,3 M,6,1 Pt,7,0 M,6,2 Pt,7,1 Pt,7,2 M,6,3 Pt,7,3 M,7,0 M,7,1 M,7,2 M,7,3"""
+ACC_BUFS = 5
+TR_BUFS = 3
+PROG = """A Is,0,256,512 Iv,0,0,256 Iv,1,0,128 Is,1,256,384 Iv,1,128,256 Is,1,384,512 Qx,0 Qx,1 S1,0,0 S1,0,1 E,0,0 Is,2,0,128 S1,0,2 S1,0,3 E,0,1 S1,1,0 Is,2,128,256 S1,1,1 E,0,2 S1,1,2 Is,2,256,384 E,0,3 S1,1,3 Is,2,384,512 E,1,0 Rs,0,0 E,1,1 Rs,0,1 E,1,2 Rs,0,2 T,0,0 E,1,3 Rs,0,3 Iv,3,0,512 G,0,0 T,0,2 Rs,1,0 Iv,5,0,128 G,0,2 Qx,3,1 Rs,1,1 Rs,1,2 T,1,0 C Qy,0 Rs,1,3 S1,2,0 Iv,7,0,128 S1,2,1 E,2,0 G,1,0 S1,2,2 S1,2,3 E,2,1 S1,3,0 Is,4,0,128 S1,3,1 E,2,2 T,1,2 Is,4,128,256 E,2,3 S1,3,2 G,1,2 S1,3,3 E,3,0 Is,4,256,384 Qy,1 Is,4,384,512 E,3,1 S2,0,0 Rs,2,0 E,3,2 S2,0,1 Rs,2,1 J,0,0 S2,0,2 Rs,2,2 J,0,1 S2,0,3 Rs,2,3 J,0,2 S2,1,0 Is,5,128,256 J,0,3 S2,1,1 Is,5,256,384 E,3,3 S2,1,2 Is,5,384,512 Qz,0 S2,1,3 Rs,3,0 J,1,0 P3,0,0 Rs,3,1 J,1,1 T,2,0 Ps,0,0 T,2,2 J,1,2 T,3,0 G,2,0 J,1,3 P3,0,1 G,2,2 Qx,5,1 P3,0,2 P3,0,3 G,3,0 Ps,0,1 Qz,1 S1,4,0 S1,4,1 Ps,0,2 E,4,0 S1,4,2 Ps,0,3 P3,1,0 E,4,1 P3,1,1 Ps,1,0 P3,1,2 E,4,2 P3,1,3 Ps,1,1 S1,4,3 Iv,7,128,256 S1,5,0 E,4,3 Ps,1,2 S1,5,1 E,5,0 Pt,0,0 Ps,1,3 Pt,0,1 M,0,0 Pt,0,2 Rs,3,2 Pt,0,3 M,0,1 Pt,1,0 Rs,3,3 M,0,2 Pt,1,1 Is,6,0,128 T,3,2 M,0,3 Is,6,128,256 Pt,1,2 M,1,0 Pt,1,3 G,3,2 M,1,1 S1,5,2 Is,6,256,384 M,1,2 S1,5,3 Is,6,384,512 M,1,3 Rs,4,0 Qy,3,1 Rs,4,1 Rs,4,2 T,4,0 E,5,1 Rs,4,3 S2,2,0 E,5,2 G,4,0 S2,2,1 E,5,3 Is,7,256,384 S2,2,2 J,2,0 Is,7,384,512 S2,2,3 J,2,1 S2,3,0 J,2,2 Rs,5,0 S2,3,1 J,2,3 Rs,5,1 S2,3,2 J,3,0 Rs,5,2 S2,3,3 Qz,2 Rs,5,3 J,3,1 T,4,2 T,5,0 J,3,2 G,4,2 T,5,2 J,3,3 G,5,0 P3,2,0 Qx,7,1 G,5,2 P3,2,1 P3,2,2 Ps,2,0 P3,2,3 Qy,5,1 Ps,2,1 S1,6,0 S1,6,1 Ps,2,2 S1,6,2 E,6,0 Ps,2,3 S1,6,3 E,6,1 S2,4,0 Rs,6,0 E,6,2 S2,4,1 Rs,6,1 Qz,3 S2,4,2 Rs,6,2 E,6,3 S2,4,3 J,4,0 Rs,6,3 P3,3,0 T,6,0 J,4,1 Ps,3,0 Pt,2,0 J,4,2 Pt,2,1 G,6,0 Pt,2,2 M,2,0 Pt,2,3 T,6,2 M,2,1 P3,3,1 G,6,2 M,2,2 P3,3,2 Ps,3,1 M,2,3 P3,3,3 Ps,3,2 S1,7,0 J,4,3 S1,7,1 Ps,3,3 S1,7,2 E,7,0 S1,7,3 E,7,1 S2,5,0 Rs,7,0 E,7,2 S2,5,1 Rs,7,1 Qz,4 S2,5,2 Rs,7,2 S2,5,3 E,7,3 J,5,0 Rs,7,3 P3,4,0 T,7,0 J,5,1 Ps,4,0 Pt,3,0 J,5,2 Pt,3,1 G,7,0 Pt,3,2 M,3,0 Pt,3,3 T,7,2 M,3,1 P3,4,1 G,7,2 M,3,2 P3,4,2 Ps,4,1 M,3,3 P3,4,3 Ps,4,2 Qy,7,1 Ps,4,3 J,5,3 Pt,4,0 Pt,4,1 M,4,0 Pt,4,2 Pt,4,3 M,4,1 S2,6,0 M,4,2 S2,6,1 M,4,3 S2,6,2 Qz,5 S2,6,3 J,6,0 S2,7,0 J,6,1 P3,5,0 J,6,2 Ps,5,0 P3,5,1 J,6,3 Ps,5,1 P3,5,2 P3,5,3 J,7,0 Ps,5,2 S2,7,1 Qz,6 Ps,5,3 S2,7,2 J,7,1 S2,7,3 J,7,2 P3,6,0 P3,6,1 Ps,6,0 P3,6,2 J,7,3 P3,6,3 Ps,6,1 Pt,5,0 Qz,7 Pt,5,1 Ps,6,2 Pt,5,2 M,5,0 Ps,6,3 Pt,5,3 M,5,1 P3,7,0 P3,7,1 M,5,2 Ps,7,0 P3,7,2 M,5,3 Ps,7,1 Pt,6,0 Pt,6,1 M,6,0 Ps,7,2 Pt,6,2 Pt,6,3 M,6,1 P3,7,3 M,6,2 Ps,7,3 M,6,3 Pt,7,0 Pt,7,1 M,7,0 Pt,7,2 Pt,7,3 M,7,1 M,7,2 M,7,3"""
 COPY = mybir.ActivationFunctionType.Copy
 
 
@@ -52,10 +52,10 @@ def tile_orchestra_bleed_mix_t2_kernel(
             return tile.bitcast(I32)
 
         nc.vector.memset(words(a_sraw[:]), 0)
-        nc.vector.memset(words(l_sc[:]), 0)
-        nc.vector.memset(words(m_sc[:]), 0)
-        nc.gpsimd.memset(resp_row[:], 0.0)
         make_identity(nc, ident[:])
+        nc.gpsimd.memset(words(l_sc[:]), 0)
+        nc.gpsimd.memset(words(m_sc[:]), 0)
+        nc.gpsimd.memset(resp_row[:], 0.0)
         make_identity(nc, ident_b[:])
 
         raws = []
@@ -94,7 +94,6 @@ def tile_orchestra_bleed_mix_t2_kernel(
         for r in range(3):
             load_rec(r)
 
-        damp_f = keep.tile([P, 4], F32)
 
         def order_a():
             nc.vector.tensor_copy(
@@ -102,7 +101,6 @@ def tile_orchestra_bleed_mix_t2_kernel(
                 in_=a_raw[:].rearrange("p (m t b) -> p t m b", t=4, b=2),
             )
             nc.vector.tensor_copy(out=a_sc[:], in_=a_sraw[:].rearrange("p (m t) -> p t m", t=4))
-            nc.vector.tensor_copy(out=damp_f[:], in_=damp_t[:])
 
         xg, xc, xs = {}, {}, {}
         et, jt, res = {}, {}, {}
@@ -162,17 +160,6 @@ def tile_orchestra_bleed_mix_t2_kernel(
                 op0=MULT,
                 op1=ADD,
             )
-
-        def bleed_s(u, t):
-            et[u, t] = work.tile([P, W], F32, name="et", bufs=2)
-            nc.scalar.activation(out=et[u, t][:], in_=acc["E", u, t][:], func=COPY, scale=damp_f[:, t : t + 1])
-
-        def bleed_g(u, t):
-            r, g = divmod(u, 2)
-            fs = slice(g * W, (g + 1) * W)
-            if r not in y:
-                y[r] = work.tile([P, 4, F], F32, align_bytes=64, name="y")
-            nc.gpsimd.tensor_tensor(out=y[r][:, t, fs], in0=et[u, t][:], in1=raws[r][:, t, fs], op=ADD)
 
         def round_y(u, t, engine):
             r, g = divmod(u, 2)
@@ -247,16 +234,6 @@ def tile_orchestra_bleed_mix_t2_kernel(
                 out=z_out, in0=acc["J", v, k][:].rearrange("p t (c i) -> p c t i", i=2), in1=y_in, op=ADD
             )
 
-        def leak_s(v, k):
-            jt[v, k] = work.tile([P, 4, P], F32, name="jt", bufs=2)
-            nc.scalar.copy(out=jt[v, k][:], in_=acc["J", v, k][:])
-
-        def leak_g(v, k):
-            z_out, y_in = leak_views(v, k)
-            nc.gpsimd.tensor_tensor(
-                out=z_out, in0=jt[v, k][:].rearrange("p t (c i) -> p c t i", i=2), in1=y_in, op=ADD
-            )
-
         def quant_z(v):
             zc[v] = work.tile([P, W], U32, align_bytes=64, name="zc")
             zs[v] = work.tile([P, W], U8, align_bytes=64, name="zs")
@@ -309,9 +286,9 @@ def tile_orchestra_bleed_mix_t2_kernel(
             "Iv": lambda u, a, b: interleave(u, "v", a, b),
             "Is": lambda u, a, b: interleave(u, "s", a, b),
             "Ig": lambda u, a, b: interleave(u, "g", a, b),
-            "Qx": quant_x, "S1": mm1, "E": bleed, "Es": bleed_s, "Eg": bleed_g,
+            "Qx": quant_x, "S1": mm1, "E": bleed,
             "Rs": lambda u, t: round_y(u, t, "s"), "Rg": lambda u, t: round_y(u, t, "g"), "T": turn1, "G": turn2,
-            "Qy": quant_y, "S2": mm2, "J": leak, "Js": leak_s, "Jg": leak_g, "Qz": quant_z, "C": columns_of_resp,
+            "Qy": quant_y, "S2": mm2, "J": leak, "Qz": quant_z, "C": columns_of_resp,
             "P3": mm3, "Ps": respond, "Pt": back, "M": record, "A": order_a,
         }
         for op in PROG.split():

@@ -12,16 +12,51 @@ E4M3 = mybir.dt.float8_e4m3fn_x4
 E2M1 = mybir.dt.float4_e2m1fn_x4
 ADD = mybir.AluOpType.add
 MULT = mybir.AluOpType.mult
+COPY = mybir.ActivationFunctionType.Copy
 
 S, T, F, C = 512, 4, 1024, 512
 P = 128
 W = 512
+HALF_FRAMES = 2 * T
 FLOPS = 2 * (2 * S * S * T * F + S * T * F * F)
 
-ACC_BUFS = 5
-TR_BUFS = 3
-PROG = """A Is,0,256,512 Iv,0,0,256 Iv,1,0,128 Is,1,256,384 Iv,1,128,256 Is,1,384,512 Qx,0 Qx,1 S1,0,0 S1,0,1 E,0,0 Is,2,0,128 S1,0,2 S1,0,3 E,0,1 S1,1,0 Is,2,128,256 S1,1,1 E,0,2 S1,1,2 Is,2,256,384 E,0,3 S1,1,3 Is,2,384,512 E,1,0 Rs,0,0 E,1,1 Rs,0,1 E,1,2 Rs,0,2 T,0,0 E,1,3 Rs,0,3 Iv,3,0,512 G,0,0 T,0,2 Rs,1,0 Iv,5,0,128 G,0,2 Qx,3,1 Rs,1,1 Rs,1,2 T,1,0 C Qy,0 Rs,1,3 S1,2,0 Iv,7,0,128 S1,2,1 E,2,0 G,1,0 S1,2,2 S1,2,3 E,2,1 S1,3,0 Is,4,0,128 S1,3,1 E,2,2 T,1,2 Is,4,128,256 E,2,3 S1,3,2 G,1,2 S1,3,3 E,3,0 Is,4,256,384 Qy,1 Is,4,384,512 E,3,1 S2,0,0 Rs,2,0 E,3,2 S2,0,1 Rs,2,1 J,0,0 S2,0,2 Rs,2,2 J,0,1 S2,0,3 Rs,2,3 J,0,2 S2,1,0 Is,5,128,256 J,0,3 S2,1,1 Is,5,256,384 E,3,3 S2,1,2 Is,5,384,512 Qz,0 S2,1,3 Rs,3,0 J,1,0 P3,0,0 Rs,3,1 J,1,1 T,2,0 Ps,0,0 T,2,2 J,1,2 T,3,0 G,2,0 J,1,3 P3,0,1 G,2,2 Qx,5,1 P3,0,2 P3,0,3 G,3,0 Ps,0,1 Qz,1 S1,4,0 S1,4,1 Ps,0,2 E,4,0 S1,4,2 Ps,0,3 P3,1,0 E,4,1 P3,1,1 Ps,1,0 P3,1,2 E,4,2 P3,1,3 Ps,1,1 S1,4,3 Iv,7,128,256 S1,5,0 E,4,3 Ps,1,2 S1,5,1 E,5,0 Pt,0,0 Ps,1,3 Pt,0,1 M,0,0 Pt,0,2 Rs,3,2 Pt,0,3 M,0,1 Pt,1,0 Rs,3,3 M,0,2 Pt,1,1 Is,6,0,128 T,3,2 M,0,3 Is,6,128,256 Pt,1,2 M,1,0 Pt,1,3 G,3,2 M,1,1 S1,5,2 Is,6,256,384 M,1,2 S1,5,3 Is,6,384,512 M,1,3 Rs,4,0 Qy,3,1 Rs,4,1 Rs,4,2 T,4,0 E,5,1 Rs,4,3 S2,2,0 E,5,2 G,4,0 S2,2,1 E,5,3 Is,7,256,384 S2,2,2 J,2,0 Is,7,384,512 S2,2,3 J,2,1 S2,3,0 J,2,2 Rs,5,0 S2,3,1 J,2,3 Rs,5,1 S2,3,2 J,3,0 Rs,5,2 S2,3,3 Qz,2 Rs,5,3 J,3,1 T,4,2 T,5,0 J,3,2 G,4,2 T,5,2 J,3,3 G,5,0 P3,2,0 Qx,7,1 G,5,2 P3,2,1 P3,2,2 Ps,2,0 P3,2,3 Qy,5,1 Ps,2,1 S1,6,0 S1,6,1 Ps,2,2 S1,6,2 E,6,0 Ps,2,3 S1,6,3 E,6,1 S2,4,0 Rs,6,0 E,6,2 S2,4,1 Rs,6,1 Qz,3 S2,4,2 Rs,6,2 E,6,3 S2,4,3 J,4,0 Rs,6,3 P3,3,0 T,6,0 J,4,1 Ps,3,0 Pt,2,0 J,4,2 Pt,2,1 G,6,0 Pt,2,2 M,2,0 Pt,2,3 T,6,2 M,2,1 P3,3,1 G,6,2 M,2,2 P3,3,2 Ps,3,1 M,2,3 P3,3,3 Ps,3,2 S1,7,0 J,4,3 S1,7,1 Ps,3,3 S1,7,2 E,7,0 S1,7,3 E,7,1 S2,5,0 Rs,7,0 E,7,2 S2,5,1 Rs,7,1 Qz,4 S2,5,2 Rs,7,2 S2,5,3 E,7,3 J,5,0 Rs,7,3 P3,4,0 T,7,0 J,5,1 Ps,4,0 Pt,3,0 J,5,2 Pt,3,1 G,7,0 Pt,3,2 M,3,0 Pt,3,3 T,7,2 M,3,1 P3,4,1 G,7,2 M,3,2 P3,4,2 Ps,4,1 M,3,3 P3,4,3 Ps,4,2 Qy,7,1 Ps,4,3 J,5,3 Pt,4,0 Pt,4,1 M,4,0 Pt,4,2 Pt,4,3 M,4,1 S2,6,0 M,4,2 S2,6,1 M,4,3 S2,6,2 Qz,5 S2,6,3 J,6,0 S2,7,0 J,6,1 P3,5,0 J,6,2 Ps,5,0 P3,5,1 J,6,3 Ps,5,1 P3,5,2 P3,5,3 J,7,0 Ps,5,2 S2,7,1 Qz,6 Ps,5,3 S2,7,2 J,7,1 S2,7,3 J,7,2 P3,6,0 P3,6,1 Ps,6,0 P3,6,2 J,7,3 P3,6,3 Ps,6,1 Pt,5,0 Qz,7 Pt,5,1 Ps,6,2 Pt,5,2 M,5,0 Ps,6,3 Pt,5,3 M,5,1 P3,7,0 P3,7,1 M,5,2 Ps,7,0 P3,7,2 M,5,3 Ps,7,1 Pt,6,0 Pt,6,1 M,6,0 Ps,7,2 Pt,6,2 Pt,6,3 M,6,1 P3,7,3 M,6,2 Ps,7,3 M,6,3 Pt,7,0 Pt,7,1 M,7,0 Pt,7,2 Pt,7,3 M,7,1 M,7,2 M,7,3"""
-COPY = mybir.ActivationFunctionType.Copy
+VECTOR_BANKS = 5
+SCALAR_BANKS = 3
+RESULTS = 8
+
+ROUND = (
+    ("interleave", (0,), 1),
+    ("add_record", (2, 3), 11),
+    ("add_record_gpsimd", (1,), 11),
+    ("respond", (0, 1), 9),
+    ("quantise_z", (0,), 8),
+    ("interleave", (1,), 0),
+    ("leak", (0, 1), 7),
+    ("copy_out", (1,), 10),
+    ("turn_y", (0,), 4),
+    ("bleed_matmul", (2, 3), 3),
+    ("round_y", (0,), 3),
+    ("add_record", (0, 1), 10),
+    ("mix_matmul", (2, 3), 9),
+    ("quantise_x", (0,), 1),
+    ("gather_y", (0,), 4),
+    ("respond", (2, 3), 9),
+    ("leak_matmul", (2, 3), 7),
+    ("bleed", (2, 3), 3),
+    ("turn_y", (2,), 4),
+    ("turn_back", (2, 3), 10),
+    ("gather_y", (2,), 4),
+    ("quantise_y", (0,), 5),
+    ("leak", (2, 3), 7),
+    ("round_y", (2,), 3),
+    ("bleed_matmul", (0, 1), 2),
+    ("mix_matmul", (0, 1), 8),
+    ("copy_out", (3,), 10),
+    ("bleed", (0, 1), 2),
+    ("leak_matmul", (0, 1), 6),
+    ("turn_back", (0, 1), 9),
+    ("add_record_gpsimd", (3,), 12),
+)
 
 
 def tile_orchestra_bleed_mix_t2_kernel(
@@ -30,267 +65,328 @@ def tile_orchestra_bleed_mix_t2_kernel(
     nc = tc.nc
     with ExitStack() as ctx:
         keep = ctx.enter_context(tc.tile_pool(name="keep", bufs=1))
-        work = ctx.enter_context(tc.tile_pool(name="work", bufs=3))
+        work = ctx.enter_context(tc.tile_pool(name="work", bufs=2))
         psum = ctx.enter_context(tc.psum_pool(name="psum", bufs=1))
         ctx.enter_context(tc.manual_schedule())
 
-        a_raw = keep.tile([P, 1024], U8, align_bytes=64)
-        a_sraw = keep.tile([P, 512], U8, align_bytes=64)
-        a_cod = keep.tile([P, 1024], U8, align_bytes=64)
-        a_sc = keep.tile([P, 4, P], U8, align_bytes=64)
-        l_cod = keep.tile([P, 2, 2 * F], U8, align_bytes=64)
-        l_sc = keep.tile([P, 2, F], U8, align_bytes=64)
-        m_cod = keep.tile([P, 2 * C], U8, align_bytes=64)
-        m_sc = keep.tile([P, C], U8, align_bytes=64)
-        damp_t = keep.tile([P, 4], BF16)
-        resp_row = keep.tile([P, P], BF16, align_bytes=64)
-        resp_c = keep.tile([P, 8], F32)
-        ident_b = keep.tile([P, P], BF16, align_bytes=64)
+        a_arrived = keep.tile([P, 2 * S], U8, align_bytes=64)
+        a_scales_arrived = keep.tile([P, S], U8, align_bytes=64)
+        a_codes = keep.tile([P, 2 * S], U8, align_bytes=64)
+        a_plane = keep.tile([P, S], U8, align_bytes=64)
+        l_codes = keep.tile([P, 2, 2 * F], U8, align_bytes=64)
+        l_plane = keep.tile([P, 2, F], U8, align_bytes=64)
+        m_codes = keep.tile([P, 2 * C], U8, align_bytes=64)
+        m_plane = keep.tile([P, C], U8, align_bytes=64)
+        damp_col = keep.tile([P, 4], BF16)
+        resp_rows = keep.tile([P, P], BF16, align_bytes=64)
+        resp_col = keep.tile([P, F // P], F32)
         ident = keep.tile([P, P], F32, align_bytes=64)
-
-        def words(tile):
-            return tile.bitcast(I32)
-
-        nc.vector.memset(words(a_sraw[:]), 0)
-        make_identity(nc, ident[:])
-        nc.gpsimd.memset(words(l_sc[:]), 0)
-        nc.gpsimd.memset(words(m_sc[:]), 0)
-        nc.gpsimd.memset(resp_row[:], 0.0)
-        make_identity(nc, ident_b[:])
-
-        raws = []
+        ident_bf16 = keep.tile([P, P], BF16, align_bytes=64)
+        raw = []
         for r in range(T):
-            raw = keep.tile([P, 4, F], BF16, align_bytes=64, name="raw%d" % r)
-            raws.append(raw)
+            raw_r = keep.tile([P, 4, F], BF16, align_bytes=64, name="raw%d" % r)
+            raw.append(raw_r)
 
-        def load_x(r, f0, f1):
-            nc.sync.dma_start(out=raws[r][:, :, f0:f1], in_=x.rearrange("(p j) r f -> p j r f", j=4)[:, :, r, f0:f1])
+        def as_int32(ap):
+            return ap.bitcast(I32)
 
-        load_x(0, 0, W)
-        nc.scalar.dma_start(out=words(a_raw[:]), in_=words(a_words[0]))
-        for q in range(4):
-            nc.scalar.dma_start(out=words(a_sraw[32 * q : 32 * q + 4, :]), in_=words(a_scales[0, 4 * q : 4 * q + 4, :]))
-        nc.scalar.dma_start(out=damp_t[:], in_=damp.rearrange("(p t) -> p t", t=4))
-        load_x(0, W, F)
-        load_x(1, 0, F)
-        nc.sync.dma_start(out=words(l_cod[:]), in_=words(l_words.rearrange("g p n -> p g n")))
-        for q in range(4):
-            nc.sync.dma_start(
-                out=words(l_sc[32 * q : 32 * q + 4, :, :]),
-                in_=words(l_scales[:, 4 * q : 4 * q + 4, :].rearrange("g q n -> q g n")),
-            )
-        load_x(2, 0, F)
-        nc.sync.dma_start(out=words(m_cod[:]), in_=words(m_words[0]))
-        for q in range(4):
-            nc.sync.dma_start(out=words(m_sc[32 * q : 32 * q + 4, :]), in_=words(m_scales[0, 4 * q : 4 * q + 4, :]))
-        nc.sync.dma_start(out=resp_row[0:8, :], in_=resp.rearrange("(b q) -> b q", q=P))
-        load_x(3, 0, F)
+        def on_gpsimd(u, m):
+            return u < 5 and m % 2 == 1
+
+        nc.vector.memset(as_int32(a_scales_arrived[:]), 0)
+        make_identity(nc, ident[:])
+        nc.gpsimd.memset(resp_rows[:], 0.0)
+        make_identity(nc, ident_bf16[:])
+        nc.gpsimd.memset(as_int32(l_plane[:]), 0)
+        nc.gpsimd.memset(as_int32(m_plane[:]), 0)
+
+        def load_x(r, f0, f1, queue=nc.sync):
+            queue.dma_start(out=raw[r][:, :, f0:f1], in_=x.rearrange("(p t) r f -> p t r f", t=4)[:, :, r, f0:f1])
+
         recs = {}
 
         def load_rec(r):
-            recs[r] = work.tile([P, 4, F], BF16, align_bytes=64, name="rec", bufs=3)
+            recs[r] = work.tile([P, C // P, F], BF16, align_bytes=64, name="rec", bufs=3)
             nc.sync.dma_start(out=recs[r][:], in_=rec.rearrange("(m c) r f -> c m r f", c=P)[:, :, r, :])
 
+        load_x(0, 0, W, nc.scalar)
+        nc.sync.dma_start(out=as_int32(a_arrived[:]), in_=as_int32(a_words[0]))
+        for q in range(4):
+            nc.sync.dma_start(
+                out=as_int32(a_scales_arrived[32 * q : 32 * q + 4, :]),
+                in_=as_int32(a_scales[0, 4 * q : 4 * q + 4, :]),
+            )
+        load_x(0, W, F)
+        nc.sync.dma_start(out=damp_col[:], in_=damp.rearrange("(p t) -> p t", t=4))
+        load_x(1, 0, F)
+        nc.sync.dma_start(out=as_int32(l_codes[:]), in_=as_int32(l_words.rearrange("g p n -> p g n")))
+        for q in range(4):
+            nc.sync.dma_start(
+                out=as_int32(l_plane[32 * q : 32 * q + 4, :, :]),
+                in_=as_int32(l_scales[:, 4 * q : 4 * q + 4, :].rearrange("g q n -> q g n")),
+            )
+        load_x(2, 0, F)
+        nc.sync.dma_start(out=resp_rows[0 : F // P, :], in_=resp.rearrange("(b q) -> b q", q=P))
+        nc.sync.dma_start(out=as_int32(m_codes[:]), in_=as_int32(m_words[0]))
+        for q in range(4):
+            nc.sync.dma_start(
+                out=as_int32(m_plane[32 * q : 32 * q + 4, :]), in_=as_int32(m_scales[0, 4 * q : 4 * q + 4, :])
+            )
+        load_x(3, 0, F)
         for r in range(3):
             load_rec(r)
 
-
-        def order_a():
+        def reorder_a(half):
+            ts = slice(2 * half, 2 * half + 2)
             nc.vector.tensor_copy(
-                out=a_cod[:].rearrange("p (t m b) -> p t m b", t=4, b=2),
-                in_=a_raw[:].rearrange("p (m t b) -> p t m b", t=4, b=2),
+                out=a_codes[:].rearrange("p (t m b) -> p t m b", t=4, b=2)[:, ts],
+                in_=a_arrived[:].rearrange("p (m t b) -> p t m b", t=4, b=2)[:, ts],
             )
-            nc.vector.tensor_copy(out=a_sc[:], in_=a_sraw[:].rearrange("p (m t) -> p t m", t=4))
+            nc.vector.tensor_copy(
+                out=a_plane[:].rearrange("p (t m) -> p t m", t=4)[:, ts],
+                in_=a_scales_arrived[:].rearrange("p (m t) -> p t m", t=4)[:, ts],
+            )
 
-        xg, xc, xs = {}, {}, {}
-        et, jt, res = {}, {}, {}
-        y, yb, yt, yc, ys = {}, {}, {}, {}, {}
-        z, zc, zs = {}, {}, {}
-        acc, tr = {}, {}
+        reorder_a(0)
 
-        def interleave(u, engine, c0, c1):
+        grouped, x_codes, x_plane = {}, {}, {}
+        y, y_bf16, y_turned, y_codes, y_plane = {}, {}, {}, {}, {}
+        z, z_codes, z_plane, scaled, copied, bank_of = {}, {}, {}, {}, {}, {}
+
+        def interleave(u, half):
             r, g = divmod(u, 2)
-            if r not in xg:
-                xg[r] = work.tile([P, 2, W, 4], BF16, align_bytes=64, name="xg", bufs=2)
-            o = xg[r][:, g, c0:c1, :].rearrange("p (c i) t -> p c t i", i=4)
-            i_ = raws[r][:, :, g * W + c0 : g * W + c1].rearrange("p t (c i) -> p c t i", i=4)
-            if engine == "v":
-                nc.vector.tensor_copy(out=o, in_=i_)
-            elif engine == "g":
-                nc.gpsimd.tensor_scalar(out=o, in0=i_, scalar1=1.0, scalar2=0.0, op0=MULT, op1=ADD)
-            else:
-                nc.scalar.copy(out=o, in_=i_)
+            if r not in grouped:
+                grouped[r] = work.tile([P, 2, W, 4], BF16, align_bytes=64, name="grouped")
+            width = W // 2 if u == 0 else W // 4
+            for f0 in range(half * W // 2, (half + 1) * W // 2, width):
+                out_ap = grouped[r][:, g, f0 : f0 + width, :]
+                in_ap = raw[r][:, :, g * W + f0 : g * W + f0 + width]
+                if half == 0 and u >= 2:
+                    nc.gpsimd.tensor_scalar(
+                        out=out_ap, in0=in_ap.rearrange("p t f -> p f t"), scalar1=1.0, scalar2=0.0, op0=MULT, op1=ADD
+                    )
+                else:
+                    copy = nc.vector.tensor_copy if (u, half) == (0, 0) else nc.scalar.copy
+                    copy(
+                        out=out_ap.rearrange("p (c i) t -> p c t i", i=4),
+                        in_=in_ap.rearrange("p t (c i) -> p c t i", i=4),
+                    )
+            if (u, half) == (0, 0):
+                reorder_a(1)
 
-        def quant_x(u, whole=0):
+        def quantise_x(u):
             r, g = divmod(u, 2)
-            gs = slice(0, 2) if whole else slice(g, g + 1)
-            if r not in xc:
-                xc[r] = work.tile([P, 2 * W], U32, align_bytes=64, name="xc", bufs=2)
-                xs[r] = work.tile([P, 2 * W], U8, align_bytes=64, name="xs", bufs=2)
-            cs = slice(gs.start * W, gs.stop * W)
+            if r not in x_codes:
+                x_codes[r] = work.tile([P, 2, W], U32, align_bytes=64, name="x_codes")
+                x_plane[r] = work.tile([P, 2, W], U8, align_bytes=64, name="x_plane")
+            if r > 0 and g == 0:
+                return
+            gs = slice(0 if r else g, g + 1)
             nc.vector.quantize_mx(
-                out=xc[r][:, cs].bitcast(E4M3),
-                scales=xs[r][:, cs],
-                in_=xg[r][:, gs].rearrange("p g w t -> p (g w t)"),
+                out=x_codes[r][:, gs, :].rearrange("p g f -> p (g f)").bitcast(E4M3),
+                scales=x_plane[r][:, gs, :].rearrange("p g f -> p (g f)"),
+                in_=grouped[r][:, gs].rearrange("p g f t -> p (g f t)"),
             )
 
-        def mm1(u, t):
-            bank = psum.tile([P, W], F32, name="acc", bufs=ACC_BUFS)
-            acc["E", u, t] = bank
+        def bleed_matmul(u, t):
+            r, g = divmod(u, 2)
+            bank = psum.tile([P, W], F32, name="for_vector", bufs=VECTOR_BANKS)
+            bank_of["bleed", u, t] = bank
             nc.tensor.matmul_mx(
                 out=bank[:],
-                lhsT=a_cod[:, 2 * P * t : 2 * P * (t + 1)].bitcast(E2M1),
-                lhsT_scale=a_sc[:, t, :],
-                rhs=xc[u // 2][:, W * (u % 2) : W * (u % 2 + 1)].bitcast(E4M3),
-                rhs_scale=xs[u // 2][:, W * (u % 2) : W * (u % 2 + 1)],
+                lhsT=a_codes[:, 2 * P * t : 2 * P * (t + 1)].bitcast(E2M1),
+                lhsT_scale=a_plane[:, P * t : P * (t + 1)],
+                rhs=x_codes[r][:, g, :].bitcast(E4M3),
+                rhs_scale=x_plane[r][:, g, :],
                 start=True,
                 stop=True,
             )
 
         def bleed(u, t):
             r, g = divmod(u, 2)
-            if r not in y:
-                y[r] = work.tile([P, 4, F], F32, align_bytes=64, name="y")
             fs = slice(g * W, (g + 1) * W)
+            if r not in y:
+                y[r] = work.tile([P, 4, F], F32, align_bytes=64, name="y", bufs=3)
             nc.vector.scalar_tensor_tensor(
                 out=y[r][:, t, fs],
-                in0=acc["E", u, t][:],
-                scalar=damp_t[:, t : t + 1],
-                in1=raws[r][:, t, fs],
+                in0=bank_of["bleed", u, t][:],
+                scalar=damp_col[:, t : t + 1],
+                in1=raw[r][:, t, fs],
                 op0=MULT,
                 op1=ADD,
             )
 
-        def round_y(u, t, engine):
+        def round_y(u, t):
             r, g = divmod(u, 2)
-            if u not in yb:
-                yb[u] = work.tile([P, 4, W], BF16, align_bytes=64, name="yb", bufs=2)
-            y_in = y[r][:, t, g * W : (g + 1) * W]
-            if engine == "s":
-                nc.scalar.copy(out=yb[u][:, t, :], in_=y_in)
-            else:
-                nc.gpsimd.tensor_scalar(out=yb[u][:, t, :], in0=y_in, scalar1=1.0, scalar2=0.0, op0=MULT, op1=ADD)
-
-        def turn1(u, t):
-            bank = tr[u, t] = psum.tile([P, 2, 2, P], F32, name="tr", bufs=TR_BUFS)
-            for tt in range(2):
-                pairs = yb[u][:, t + tt, :].bitcast(F32)
-                for h in range(2):
-                    nc.tensor.transpose(bank[:, tt, h, :], pairs[:, h:256:2], ident[:])
-
-        def turn2(u, t):
-            r, g = divmod(u, 2)
-            if r not in yt:
-                yt[r] = work.tile([P, 2 * 4 * 512], BF16, align_bytes=64, name="yt", bufs=2)
+            if u not in y_bf16:
+                y_bf16[u] = work.tile([P, 4 * W], BF16, align_bytes=64, name="y_bf16")
             nc.scalar.copy(
-                out=yt[r][:].bitcast(F32).rearrange("p (g t j h) -> p g t j h", g=2, t=4, h=2)[:, g, t : t + 2],
-                in_=tr[u, t][:].rearrange("p t h j -> p t j h"),
+                out=y_bf16[u][:, W * t : W * (t + 2)].rearrange("p (t h w e) -> p t h w e", t=2, h=2, e=2),
+                in_=y[r][:, t : t + 2, g * W : (g + 1) * W].rearrange("p t (w h e) -> p t h w e", h=2, e=2),
             )
 
-        def quant_y(u, whole=0):
-            r, g = divmod(u, 2)
-            if r not in yc:
-                yc[r] = work.tile([P, 2, 512], U32, align_bytes=64, name="yc", bufs=2)
-                ys[r] = work.tile([P, 2, 512], U8, align_bytes=64, name="ys", bufs=2)
-            if whole:
-                nc.vector.quantize_mx(
-                    out=yc[r][:].rearrange("p g j -> p (g j)").bitcast(E4M3),
-                    scales=ys[r][:].rearrange("p g j -> p (g j)"),
-                    in_=yt[r][:],
-                )
-            else:
-                nc.vector.quantize_mx(
-                    out=yc[r][:, g, :].bitcast(E4M3), scales=ys[r][:, g, :], in_=yt[r][:, 2048 * g : 2048 * (g + 1)]
-                )
+        def turn_y(u, t):
+            bank = psum.tile([P, 2, 2, P], F32, name="for_scalar", bufs=SCALAR_BANKS)
+            bank_of["turn", u, t] = bank
+            for dt in range(2):
+                for h in range(2):
+                    first = W * (t + dt) + W // 2 * h
+                    pairs = y_bf16[u][:, first : first + W // 2].bitcast(F32)
+                    nc.tensor.transpose(bank[:, dt, h, :], pairs, ident[:])
 
-        def mm2(v, k):
-            r, b = v // 2, 4 * (v % 2) + k
-            bank = psum.tile([P, 4, P], F32, name="acc", bufs=ACC_BUFS)
-            acc["J", v, k] = bank
+        def gather_y(u, t):
+            r, g = divmod(u, 2)
+            if r not in y_turned:
+                y_turned[r] = work.tile([P, 2 * 4 * S], BF16, align_bytes=64, name="y_turned")
+            pairs = y_turned[r][:].bitcast(F32).rearrange("p (g t j h) -> p g t j h", g=2, t=4, h=2)
+            nc.scalar.copy(
+                out=pairs[:, g, t : t + 2], in_=bank_of["turn", u, t][:].rearrange("p t h j -> p t j h")
+            )
+
+        def quantise_y(u):
+            r, g = divmod(u, 2)
+            if r not in y_codes:
+                y_codes[r] = work.tile([P, 2, S], U32, align_bytes=64, name="y_codes")
+                y_plane[r] = work.tile([P, 2, S], U8, align_bytes=64, name="y_plane")
+            if r > 0 and g == 0:
+                return
+            gs = slice(0 if r else g, g + 1)
+            nc.vector.quantize_mx(
+                out=y_codes[r][:, gs, :].rearrange("p g j -> p (g j)").bitcast(E4M3),
+                scales=y_plane[r][:, gs, :].rearrange("p g j -> p (g j)"),
+                in_=y_turned[r][:, 4 * S * gs.start : 4 * S * gs.stop],
+            )
+
+        def leak_matmul(u, k):
+            r, b = u // 2, 4 * (u % 2) + k
+            bank = psum.tile([P, 4, P], F32, name="for_vector", bufs=VECTOR_BANKS)
+            bank_of["leak", u, k] = bank
             for t in range(4):
                 for g in range(2):
                     nc.tensor.matmul_mx(
                         out=bank[:, t, :],
-                        lhsT=yc[r][:, g, t * P : (t + 1) * P].bitcast(E4M3),
-                        lhsT_scale=ys[r][:, g, t * P : (t + 1) * P],
-                        rhs=l_cod[:, g, 2 * P * b : 2 * P * (b + 1)].bitcast(E2M1),
-                        rhs_scale=l_sc[:, g, P * b : P * (b + 1)],
+                        lhsT=y_codes[r][:, g, P * t : P * (t + 1)].bitcast(E4M3),
+                        lhsT_scale=y_plane[r][:, g, P * t : P * (t + 1)],
+                        rhs=l_codes[:, g, 2 * P * b : 2 * P * (b + 1)].bitcast(E2M1),
+                        rhs_scale=l_plane[:, g, P * b : P * (b + 1)],
                         start=(g == 0),
                         stop=(g == 1),
                     )
 
-        def leak_views(v, k):
-            r, g = divmod(v, 2)
-            b = 4 * g + k
-            if v not in z:
-                z[v] = work.tile([P, W, 4], BF16, align_bytes=64, name="z")
-            z_out = z[v][:, P * k : P * (k + 1), :].rearrange("p (c i) t -> p c t i", i=2)
-            y_in = y[r][:, :, P * b : P * (b + 1)].rearrange("p t (c i) -> p c t i", i=2)
-            return z_out, y_in
-
-        def leak(v, k):
-            z_out, y_in = leak_views(v, k)
+        def leak(u, k):
+            r, b = u // 2, 4 * (u % 2) + k
+            if u not in z:
+                z[u] = work.tile([P, W, 4], BF16, align_bytes=64, name="z", bufs=3)
             nc.vector.tensor_tensor(
-                out=z_out, in0=acc["J", v, k][:].rearrange("p t (c i) -> p c t i", i=2), in1=y_in, op=ADD
+                out=z[u][:, P * k : P * (k + 1), :].rearrange("p (c i) t -> p c t i", i=2),
+                in0=bank_of["leak", u, k][:].rearrange("p t (c i) -> p c t i", i=2),
+                in1=y[r][:, :, P * b : P * (b + 1)].rearrange("p t (c i) -> p c t i", i=2),
+                op=ADD,
             )
 
-        def quant_z(v):
-            zc[v] = work.tile([P, W], U32, align_bytes=64, name="zc")
-            zs[v] = work.tile([P, W], U8, align_bytes=64, name="zs")
+        def quantise_z(u):
+            z_codes[u] = work.tile([P, W], U32, align_bytes=64, name="z_codes", bufs=3)
+            z_plane[u] = work.tile([P, W], U8, align_bytes=64, name="z_plane", bufs=3)
             nc.vector.quantize_mx(
-                out=zc[v][:].bitcast(E4M3), scales=zs[v][:], in_=z[v][:].rearrange("p f t -> p (f t)")
+                out=z_codes[u][:].bitcast(E4M3), scales=z_plane[u][:], in_=z[u][:].rearrange("p f t -> p (f t)")
             )
 
-        def columns_of_resp():
-            bank = psum.tile([P, P], BF16, name="tr", bufs=TR_BUFS)
-            nc.tensor.transpose(bank[:], resp_row[:], ident_b[:])
-            nc.vector.tensor_copy(out=resp_c[:], in_=bank[:, 0:8])
+        def turn_resp():
+            bank = psum.tile([P, P], BF16, name="for_scalar", bufs=SCALAR_BANKS)
+            nc.tensor.transpose(bank[:], resp_rows[:], ident_bf16[:])
+            nc.scalar.copy(out=resp_col[:], in_=bank[:, 0 : F // P])
 
-        def mm3(v, k):
-            bank = psum.tile([P, C], F32, name="acc", bufs=ACC_BUFS)
-            acc["P", v, k] = bank
+        def mix_matmul(u, k):
+            if (u, k) == (0, 0):
+                turn_resp()
+            bank = psum.tile([P, C], F32, name="for_scalar", bufs=SCALAR_BANKS)
+            bank_of["mix", u, k] = bank
             nc.tensor.matmul_mx(
                 out=bank[:],
-                lhsT=zc[v][:, P * k : P * (k + 1)].bitcast(E4M3),
-                lhsT_scale=zs[v][:, P * k : P * (k + 1)],
-                rhs=m_cod[:].bitcast(E2M1),
-                rhs_scale=m_sc[:],
+                lhsT=z_codes[u][:, P * k : P * (k + 1)].bitcast(E4M3),
+                lhsT_scale=z_plane[u][:, P * k : P * (k + 1)],
+                rhs=m_codes[:].bitcast(E2M1),
+                rhs_scale=m_plane[:],
                 start=True,
                 stop=True,
             )
 
-        def respond(v, k):
-            if v not in res:
-                res[v] = work.tile([P, 4, C], F32, align_bytes=64, name="res", bufs=2)
-            b = 4 * (v % 2) + k
-            nc.scalar.activation(out=res[v][:, k, :], in_=acc["P", v, k][:], func=COPY, scale=resp_c[:, b : b + 1])
-
-        def back(v, m):
-            bank = psum.tile([P, 4, P], F32, name="acc", bufs=ACC_BUFS)
-            acc["M", v, m] = bank
-            for k in range(4):
-                nc.tensor.transpose(bank[:, k, :], res[v][:, k, P * m : P * (m + 1)], ident[:])
-
-        def record(v, m):
-            r, g = divmod(v, 2)
-            fs = slice(g * W, (g + 1) * W)
-            fin = work.tile([P, W], F32, name="fin", bufs=6)
-            nc.vector.tensor_tensor(
-                out=fin[:], in0=acc["M", v, m][:].rearrange("p k f -> p (k f)"), in1=recs[r][:, m, fs], op=ADD
+        def respond(u, k):
+            if u not in scaled:
+                scaled[u] = work.tile([P, 4, C], F32, align_bytes=64, name="scaled")
+            b = 4 * (u % 2) + k
+            nc.scalar.activation(
+                out=scaled[u][:, k, :], in_=bank_of["mix", u, k][:], func=COPY, scale=resp_col[:, b : b + 1]
             )
-            nc.sync.dma_start(out=out[m * P : (m + 1) * P, r, fs], in_=fin[:])
-            if (v, m) == (2, 0):
+
+        def turn_back(u, m):
+            if on_gpsimd(u, m):
+                bank = psum.tile([P, 4, P], F32, name="for_scalar", bufs=SCALAR_BANKS)
+            else:
+                bank = psum.tile([P, 4, P], F32, name="for_vector", bufs=VECTOR_BANKS)
+            bank_of["back", u, m] = bank
+            for k in range(4):
+                nc.tensor.transpose(bank[:, k, :], scaled[u][:, k, P * m : P * (m + 1)], ident[:])
+
+        def store(u, m, result):
+            r, g = divmod(u, 2)
+            nc.sync.dma_start(out=out[P * m : P * (m + 1), r, g * W : (g + 1) * W], in_=result[:])
+            if u == 3 and 3 not in recs:
                 load_rec(3)
 
-        do = {
-            "Iv": lambda u, a, b: interleave(u, "v", a, b),
-            "Is": lambda u, a, b: interleave(u, "s", a, b),
-            "Ig": lambda u, a, b: interleave(u, "g", a, b),
-            "Qx": quant_x, "S1": mm1, "E": bleed,
-            "Rs": lambda u, t: round_y(u, t, "s"), "Rg": lambda u, t: round_y(u, t, "g"), "T": turn1, "G": turn2,
-            "Qy": quant_y, "S2": mm2, "J": leak, "Qz": quant_z, "C": columns_of_resp,
-            "P3": mm3, "Ps": respond, "Pt": back, "M": record, "A": order_a,
+        def copy_out(u, m):
+            if on_gpsimd(u, m):
+                copied[u, m] = work.tile([P, W], F32, name="copied", bufs=3)
+                nc.scalar.copy(out=copied[u, m][:], in_=bank_of["back", u, m][:].rearrange("p k f -> p (k f)"))
+
+        def add_record_gpsimd(u, m):
+            if on_gpsimd(u, m):
+                r, g = divmod(u, 2)
+                result = work.tile([P, W], F32, name="result", bufs=RESULTS)
+                for f0 in range(0, W, W // 2):
+                    nc.gpsimd.tensor_tensor(
+                        out=result[:, f0 : f0 + W // 2],
+                        in0=copied[u, m][:, f0 : f0 + W // 2],
+                        in1=recs[r][:, m, g * W + f0 : g * W + f0 + W // 2],
+                        op=ADD,
+                    )
+                store(u, m, result)
+
+        def add_record(u, m):
+            if on_gpsimd(u, m):
+                return
+            r, g = divmod(u, 2)
+            result = work.tile([P, W], F32, name="result", bufs=RESULTS)
+            nc.vector.tensor_tensor(
+                out=result[:],
+                in0=bank_of["back", u, m][:].rearrange("p k f -> p (k f)"),
+                in1=recs[r][:, m, g * W : (g + 1) * W],
+                op=ADD,
+            )
+            store(u, m, result)
+
+        stages = {
+            "interleave": interleave,
+            "quantise_x": lambda u, i: quantise_x(u),
+            "bleed_matmul": bleed_matmul,
+            "bleed": bleed,
+            "round_y": round_y,
+            "turn_y": turn_y,
+            "gather_y": gather_y,
+            "quantise_y": lambda u, i: quantise_y(u),
+            "leak_matmul": leak_matmul,
+            "leak": leak,
+            "quantise_z": lambda u, i: quantise_z(u),
+            "mix_matmul": mix_matmul,
+            "respond": respond,
+            "turn_back": turn_back,
+            "add_record": add_record,
+            "copy_out": copy_out,
+            "add_record_gpsimd": add_record_gpsimd,
         }
-        for op in PROG.split():
-            parts = op.split(",")
-            do[parts[0]](*[int(q) for q in parts[1:]])
+        last_lag = max(lag for stage, steps, lag in ROUND)
+        for h in range(HALF_FRAMES + last_lag):
+            for stage, steps, lag in ROUND:
+                if 0 <= h - lag < HALF_FRAMES:
+                    for i in steps:
+                        stages[stage](h - lag, i)

from contextlib import ExitStack

import concourse.mybir as mybir
from concourse.masks import make_identity

F32 = mybir.dt.float32
BF16 = mybir.dt.bfloat16
U32 = mybir.dt.uint32
I32 = mybir.dt.int32
U8 = mybir.dt.uint8
E4M3 = mybir.dt.float8_e4m3fn_x4
E2M1 = mybir.dt.float4_e2m1fn_x4
ADD = mybir.AluOpType.add
MULT = mybir.AluOpType.mult
COPY = mybir.ActivationFunctionType.Copy

S, T, F, C = 512, 4, 1024, 512
P = 128
W = 512
HALF_FRAMES = 2 * T
FLOPS = 2 * (2 * S * S * T * F + S * T * F * F)

VECTOR_BANKS = 5
SCALAR_BANKS = 3
RESULTS = 8

ROUND = (
    ("interleave", (0,), 1),
    ("add_record", (2, 3), 11),
    ("add_record_gpsimd", (1,), 11),
    ("respond", (0, 1), 9),
    ("quantise_z", (0,), 8),
    ("interleave", (1,), 0),
    ("leak", (0, 1), 7),
    ("copy_out", (1,), 10),
    ("turn_y", (0,), 4),
    ("bleed_matmul", (2, 3), 3),
    ("round_y", (0,), 3),
    ("add_record", (0, 1), 10),
    ("mix_matmul", (2, 3), 9),
    ("quantise_x", (0,), 1),
    ("gather_y", (0,), 4),
    ("respond", (2, 3), 9),
    ("leak_matmul", (2, 3), 7),
    ("bleed", (2, 3), 3),
    ("turn_y", (2,), 4),
    ("turn_back", (2, 3), 10),
    ("gather_y", (2,), 4),
    ("quantise_y", (0,), 5),
    ("leak", (2, 3), 7),
    ("round_y", (2,), 3),
    ("bleed_matmul", (0, 1), 2),
    ("mix_matmul", (0, 1), 8),
    ("copy_out", (3,), 10),
    ("bleed", (0, 1), 2),
    ("leak_matmul", (0, 1), 6),
    ("turn_back", (0, 1), 9),
    ("add_record_gpsimd", (3,), 12),
)


def tile_orchestra_bleed_mix_t2_kernel(
    tc, x, a_words, a_scales, l_words, l_scales, m_words, m_scales, damp, resp, rec, out
):
    nc = tc.nc
    with ExitStack() as ctx:
        keep = ctx.enter_context(tc.tile_pool(name="keep", bufs=1))
        work = ctx.enter_context(tc.tile_pool(name="work", bufs=2))
        psum = ctx.enter_context(tc.psum_pool(name="psum", bufs=1))
        ctx.enter_context(tc.manual_schedule())

        a_arrived = keep.tile([P, 2 * S], U8, align_bytes=64)
        a_scales_arrived = keep.tile([P, S], U8, align_bytes=64)
        a_codes = keep.tile([P, 2 * S], U8, align_bytes=64)
        a_plane = keep.tile([P, S], U8, align_bytes=64)
        l_codes = keep.tile([P, 2, 2 * F], U8, align_bytes=64)
        l_plane = keep.tile([P, 2, F], U8, align_bytes=64)
        m_codes = keep.tile([P, 2 * C], U8, align_bytes=64)
        m_plane = keep.tile([P, C], U8, align_bytes=64)
        damp_col = keep.tile([P, 4], BF16)
        resp_rows = keep.tile([P, P], BF16, align_bytes=64)
        resp_col = keep.tile([P, F // P], F32)
        ident = keep.tile([P, P], F32, align_bytes=64)
        ident_bf16 = keep.tile([P, P], BF16, align_bytes=64)
        raw = []
        for r in range(T):
            raw_r = keep.tile([P, 4, F], BF16, align_bytes=64, name="raw%d" % r)
            raw.append(raw_r)

        def as_int32(ap):
            return ap.bitcast(I32)

        def on_gpsimd(u, m):
            return u < 5 and m % 2 == 1

        nc.vector.memset(as_int32(a_scales_arrived[:]), 0)
        make_identity(nc, ident[:])
        nc.gpsimd.memset(resp_rows[:], 0.0)
        make_identity(nc, ident_bf16[:])
        nc.gpsimd.memset(as_int32(l_plane[:]), 0)
        nc.gpsimd.memset(as_int32(m_plane[:]), 0)

        def load_x(r, f0, f1, queue=nc.sync):
            queue.dma_start(out=raw[r][:, :, f0:f1], in_=x.rearrange("(p t) r f -> p t r f", t=4)[:, :, r, f0:f1])

        recs = {}

        def load_rec(r):
            recs[r] = work.tile([P, C // P, F], BF16, align_bytes=64, name="rec", bufs=3)
            nc.sync.dma_start(out=recs[r][:], in_=rec.rearrange("(m c) r f -> c m r f", c=P)[:, :, r, :])

        load_x(0, 0, W, nc.scalar)
        nc.sync.dma_start(out=as_int32(a_arrived[:]), in_=as_int32(a_words[0]))
        for q in range(4):
            nc.sync.dma_start(
                out=as_int32(a_scales_arrived[32 * q : 32 * q + 4, :]),
                in_=as_int32(a_scales[0, 4 * q : 4 * q + 4, :]),
            )
        load_x(0, W, F)
        nc.sync.dma_start(out=damp_col[:], in_=damp.rearrange("(p t) -> p t", t=4))
        load_x(1, 0, F)
        nc.sync.dma_start(out=as_int32(l_codes[:]), in_=as_int32(l_words.rearrange("g p n -> p g n")))
        for q in range(4):
            nc.sync.dma_start(
                out=as_int32(l_plane[32 * q : 32 * q + 4, :, :]),
                in_=as_int32(l_scales[:, 4 * q : 4 * q + 4, :].rearrange("g q n -> q g n")),
            )
        load_x(2, 0, F)
        nc.sync.dma_start(out=resp_rows[0 : F // P, :], in_=resp.rearrange("(b q) -> b q", q=P))
        nc.sync.dma_start(out=as_int32(m_codes[:]), in_=as_int32(m_words[0]))
        for q in range(4):
            nc.sync.dma_start(
                out=as_int32(m_plane[32 * q : 32 * q + 4, :]), in_=as_int32(m_scales[0, 4 * q : 4 * q + 4, :])
            )
        load_x(3, 0, F)
        for r in range(3):
            load_rec(r)

        def reorder_a(half):
            ts = slice(2 * half, 2 * half + 2)
            nc.vector.tensor_copy(
                out=a_codes[:].rearrange("p (t m b) -> p t m b", t=4, b=2)[:, ts],
                in_=a_arrived[:].rearrange("p (m t b) -> p t m b", t=4, b=2)[:, ts],
            )
            nc.vector.tensor_copy(
                out=a_plane[:].rearrange("p (t m) -> p t m", t=4)[:, ts],
                in_=a_scales_arrived[:].rearrange("p (m t) -> p t m", t=4)[:, ts],
            )

        reorder_a(0)

        grouped, x_codes, x_plane = {}, {}, {}
        y, y_bf16, y_turned, y_codes, y_plane = {}, {}, {}, {}, {}
        z, z_codes, z_plane, scaled, copied, bank_of = {}, {}, {}, {}, {}, {}

        def interleave(u, half):
            r, g = divmod(u, 2)
            if r not in grouped:
                grouped[r] = work.tile([P, 2, W, 4], BF16, align_bytes=64, name="grouped")
            width = W // 2 if u == 0 else W // 4
            for f0 in range(half * W // 2, (half + 1) * W // 2, width):
                out_ap = grouped[r][:, g, f0 : f0 + width, :]
                in_ap = raw[r][:, :, g * W + f0 : g * W + f0 + width]
                if half == 0 and u >= 2:
                    nc.gpsimd.tensor_scalar(
                        out=out_ap, in0=in_ap.rearrange("p t f -> p f t"), scalar1=1.0, scalar2=0.0, op0=MULT, op1=ADD
                    )
                else:
                    copy = nc.vector.tensor_copy if (u, half) == (0, 0) else nc.scalar.copy
                    copy(
                        out=out_ap.rearrange("p (c i) t -> p c t i", i=4),
                        in_=in_ap.rearrange("p t (c i) -> p c t i", i=4),
                    )
            if (u, half) == (0, 0):
                reorder_a(1)

        def quantise_x(u):
            r, g = divmod(u, 2)
            if r not in x_codes:
                x_codes[r] = work.tile([P, 2, W], U32, align_bytes=64, name="x_codes")
                x_plane[r] = work.tile([P, 2, W], U8, align_bytes=64, name="x_plane")
            if r > 0 and g == 0:
                return
            gs = slice(0 if r else g, g + 1)
            nc.vector.quantize_mx(
                out=x_codes[r][:, gs, :].rearrange("p g f -> p (g f)").bitcast(E4M3),
                scales=x_plane[r][:, gs, :].rearrange("p g f -> p (g f)"),
                in_=grouped[r][:, gs].rearrange("p g f t -> p (g f t)"),
            )

        def bleed_matmul(u, t):
            r, g = divmod(u, 2)
            bank = psum.tile([P, W], F32, name="for_vector", bufs=VECTOR_BANKS)
            bank_of["bleed", u, t] = bank
            nc.tensor.matmul_mx(
                out=bank[:],
                lhsT=a_codes[:, 2 * P * t : 2 * P * (t + 1)].bitcast(E2M1),
                lhsT_scale=a_plane[:, P * t : P * (t + 1)],
                rhs=x_codes[r][:, g, :].bitcast(E4M3),
                rhs_scale=x_plane[r][:, g, :],
                start=True,
                stop=True,
            )

        def bleed(u, t):
            r, g = divmod(u, 2)
            fs = slice(g * W, (g + 1) * W)
            if r not in y:
                y[r] = work.tile([P, 4, F], F32, align_bytes=64, name="y", bufs=3)
            nc.vector.scalar_tensor_tensor(
                out=y[r][:, t, fs],
                in0=bank_of["bleed", u, t][:],
                scalar=damp_col[:, t : t + 1],
                in1=raw[r][:, t, fs],
                op0=MULT,
                op1=ADD,
            )

        def round_y(u, t):
            r, g = divmod(u, 2)
            if u not in y_bf16:
                y_bf16[u] = work.tile([P, 4 * W], BF16, align_bytes=64, name="y_bf16")
            nc.scalar.copy(
                out=y_bf16[u][:, W * t : W * (t + 2)].rearrange("p (t h w e) -> p t h w e", t=2, h=2, e=2),
                in_=y[r][:, t : t + 2, g * W : (g + 1) * W].rearrange("p t (w h e) -> p t h w e", h=2, e=2),
            )

        def turn_y(u, t):
            bank = psum.tile([P, 2, 2, P], F32, name="for_scalar", bufs=SCALAR_BANKS)
            bank_of["turn", u, t] = bank
            for dt in range(2):
                for h in range(2):
                    first = W * (t + dt) + W // 2 * h
                    pairs = y_bf16[u][:, first : first + W // 2].bitcast(F32)
                    nc.tensor.transpose(bank[:, dt, h, :], pairs, ident[:])

        def gather_y(u, t):
            r, g = divmod(u, 2)
            if r not in y_turned:
                y_turned[r] = work.tile([P, 2 * 4 * S], BF16, align_bytes=64, name="y_turned")
            pairs = y_turned[r][:].bitcast(F32).rearrange("p (g t j h) -> p g t j h", g=2, t=4, h=2)
            nc.scalar.copy(
                out=pairs[:, g, t : t + 2], in_=bank_of["turn", u, t][:].rearrange("p t h j -> p t j h")
            )

        def quantise_y(u):
            r, g = divmod(u, 2)
            if r not in y_codes:
                y_codes[r] = work.tile([P, 2, S], U32, align_bytes=64, name="y_codes")
                y_plane[r] = work.tile([P, 2, S], U8, align_bytes=64, name="y_plane")
            if r > 0 and g == 0:
                return
            gs = slice(0 if r else g, g + 1)
            nc.vector.quantize_mx(
                out=y_codes[r][:, gs, :].rearrange("p g j -> p (g j)").bitcast(E4M3),
                scales=y_plane[r][:, gs, :].rearrange("p g j -> p (g j)"),
                in_=y_turned[r][:, 4 * S * gs.start : 4 * S * gs.stop],
            )

        def leak_matmul(u, k):
            r, b = u // 2, 4 * (u % 2) + k
            bank = psum.tile([P, 4, P], F32, name="for_vector", bufs=VECTOR_BANKS)
            bank_of["leak", u, k] = bank
            for t in range(4):
                for g in range(2):
                    nc.tensor.matmul_mx(
                        out=bank[:, t, :],
                        lhsT=y_codes[r][:, g, P * t : P * (t + 1)].bitcast(E4M3),
                        lhsT_scale=y_plane[r][:, g, P * t : P * (t + 1)],
                        rhs=l_codes[:, g, 2 * P * b : 2 * P * (b + 1)].bitcast(E2M1),
                        rhs_scale=l_plane[:, g, P * b : P * (b + 1)],
                        start=(g == 0),
                        stop=(g == 1),
                    )

        def leak(u, k):
            r, b = u // 2, 4 * (u % 2) + k
            if u not in z:
                z[u] = work.tile([P, W, 4], BF16, align_bytes=64, name="z", bufs=3)
            nc.vector.tensor_tensor(
                out=z[u][:, P * k : P * (k + 1), :].rearrange("p (c i) t -> p c t i", i=2),
                in0=bank_of["leak", u, k][:].rearrange("p t (c i) -> p c t i", i=2),
                in1=y[r][:, :, P * b : P * (b + 1)].rearrange("p t (c i) -> p c t i", i=2),
                op=ADD,
            )

        def quantise_z(u):
            z_codes[u] = work.tile([P, W], U32, align_bytes=64, name="z_codes", bufs=3)
            z_plane[u] = work.tile([P, W], U8, align_bytes=64, name="z_plane", bufs=3)
            nc.vector.quantize_mx(
                out=z_codes[u][:].bitcast(E4M3), scales=z_plane[u][:], in_=z[u][:].rearrange("p f t -> p (f t)")
            )

        def turn_resp():
            bank = psum.tile([P, P], BF16, name="for_scalar", bufs=SCALAR_BANKS)
            nc.tensor.transpose(bank[:], resp_rows[:], ident_bf16[:])
            nc.scalar.copy(out=resp_col[:], in_=bank[:, 0 : F // P])

        def mix_matmul(u, k):
            if (u, k) == (0, 0):
                turn_resp()
            bank = psum.tile([P, C], F32, name="for_scalar", bufs=SCALAR_BANKS)
            bank_of["mix", u, k] = bank
            nc.tensor.matmul_mx(
                out=bank[:],
                lhsT=z_codes[u][:, P * k : P * (k + 1)].bitcast(E4M3),
                lhsT_scale=z_plane[u][:, P * k : P * (k + 1)],
                rhs=m_codes[:].bitcast(E2M1),
                rhs_scale=m_plane[:],
                start=True,
                stop=True,
            )

        def respond(u, k):
            if u not in scaled:
                scaled[u] = work.tile([P, 4, C], F32, align_bytes=64, name="scaled")
            b = 4 * (u % 2) + k
            nc.scalar.activation(
                out=scaled[u][:, k, :], in_=bank_of["mix", u, k][:], func=COPY, scale=resp_col[:, b : b + 1]
            )

        def turn_back(u, m):
            if on_gpsimd(u, m):
                bank = psum.tile([P, 4, P], F32, name="for_scalar", bufs=SCALAR_BANKS)
            else:
                bank = psum.tile([P, 4, P], F32, name="for_vector", bufs=VECTOR_BANKS)
            bank_of["back", u, m] = bank
            for k in range(4):
                nc.tensor.transpose(bank[:, k, :], scaled[u][:, k, P * m : P * (m + 1)], ident[:])

        def store(u, m, result):
            r, g = divmod(u, 2)
            nc.sync.dma_start(out=out[P * m : P * (m + 1), r, g * W : (g + 1) * W], in_=result[:])
            if u == 3 and 3 not in recs:
                load_rec(3)

        def copy_out(u, m):
            if on_gpsimd(u, m):
                copied[u, m] = work.tile([P, W], F32, name="copied", bufs=3)
                nc.scalar.copy(out=copied[u, m][:], in_=bank_of["back", u, m][:].rearrange("p k f -> p (k f)"))

        def add_record_gpsimd(u, m):
            if on_gpsimd(u, m):
                r, g = divmod(u, 2)
                result = work.tile([P, W], F32, name="result", bufs=RESULTS)
                for f0 in range(0, W, W // 2):
                    nc.gpsimd.tensor_tensor(
                        out=result[:, f0 : f0 + W // 2],
                        in0=copied[u, m][:, f0 : f0 + W // 2],
                        in1=recs[r][:, m, g * W + f0 : g * W + f0 + W // 2],
                        op=ADD,
                    )
                store(u, m, result)

        def add_record(u, m):
            if on_gpsimd(u, m):
                return
            r, g = divmod(u, 2)
            result = work.tile([P, W], F32, name="result", bufs=RESULTS)
            nc.vector.tensor_tensor(
                out=result[:],
                in0=bank_of["back", u, m][:].rearrange("p k f -> p (k f)"),
                in1=recs[r][:, m, g * W : (g + 1) * W],
                op=ADD,
            )
            store(u, m, result)

        stages = {
            "interleave": interleave,
            "quantise_x": lambda u, i: quantise_x(u),
            "bleed_matmul": bleed_matmul,
            "bleed": bleed,
            "round_y": round_y,
            "turn_y": turn_y,
            "gather_y": gather_y,
            "quantise_y": lambda u, i: quantise_y(u),
            "leak_matmul": leak_matmul,
            "leak": leak,
            "quantise_z": lambda u, i: quantise_z(u),
            "mix_matmul": mix_matmul,
            "respond": respond,
            "turn_back": turn_back,
            "add_record": add_record,
            "copy_out": copy_out,
            "add_record_gpsimd": add_record_gpsimd,
        }
        last_lag = max(lag for stage, steps, lag in ROUND)
        for h in range(HALF_FRAMES + last_lag):
            for stage, steps, lag in ROUND:
                if 0 <= h - lag < HALF_FRAMES:
                    for i in steps:
                        stages[stage](h - lag, i)
